import numpy as np, ml_dtypes
CORES = [24,25,26,27,28,29,30,31]
N = 8
BF = ml_dtypes.bfloat16
def f(rng, *shape):
    return (rng.standard_normal(shape, dtype=np.float32) * np.exp2(rng.integers(-2, 3, shape[:-1] + (1,)))).astype(BF)
def wide(rng, *shape):
    v = f(rng, *shape).astype(np.float32); k = shape[:-2] + (1, shape[-1])
    return (v * np.exp2(rng.integers(-6, 7, k)) * (rng.random(k) > 0.0625)).astype(BF)
def gentries(a):
    return np.ascontiguousarray(a.reshape(8, 16, -1).transpose(0, 2, 1)).reshape(8, -1)
def gtable(e):
    e = np.asarray(e); return np.ascontiguousarray(e.reshape(8, -1, 16).transpose(0, 2, 1)).reshape(128, -1).astype(np.int32)
NV, NC, E, B, CX, A, KN = 3072, 1024, 2048, 128, 64, 256, 16
def lists8(a):
    return np.stack([gentries(v) for v in a])
def tables8(e):
    return np.stack([gtable(v) for v in e])
def cases(s, cor):
    t = np.take_along_axis(s, lists8(cor), -1).reshape(N, 8, 8, NC).astype(np.int64)
    return np.sum(t << np.arange(8)[:, None], axis=2)
def crossings(s, bl):
    w = np.take_along_axis(s, lists8(bl), -1).reshape(N, 8, N, B).transpose(0, 2, 1, 3)
    return w != w.transpose(1, 0, 2, 3)
def pick(rng, s, want, h):
    o = np.argsort(s, axis=-1, kind="stable"); n0 = NV - np.sum(s, axis=-1, keepdims=True)
    u = rng.integers(0, 4, want.shape) * 0.25 if h else rng.random(want.shape)
    i = np.where(want, n0 + np.minimum(np.floor(u * (NV - n0)), NV - n0 - 1), np.minimum(np.floor(u * n0), n0 - 1)).astype(np.int64)
    return np.take_along_axis(o, i, -1)
def make(rng, act, cross, zero=0.0625, h=False):
    s = rng.random((N, 8, NV)) < rng.uniform(0.3, 0.7, (N, 8, 1))
    m = (rng.random(s.shape) + 0.0625) * np.exp2(rng.integers(-3, 4, s.shape))
    z = np.where(rng.random(s.shape) < 0.5, 0.0, -0.0)
    lv = np.where(s, -m, np.where(rng.random(s.shape) < zero, z, m)).astype(BF)
    key = rng.random((N, 8, NC)); key[..., 0] -= rng.integers(0, 2, (N, 8)); key[..., -1] -= rng.integers(0, 2, (N, 8))
    on = (np.argsort(np.argsort(key, axis=-1), axis=-1) < act[..., None])[:, :, None]
    k = np.arange(8)[:, None]; c1 = rng.integers(0, 8, (N, 8, 1, NC)); c2 = (c1 + rng.integers(1, 8, c1.shape)) % 8
    w = (rng.random((N, 8, 8, NC)) < 0.5) & (k != c2) | (k == c1)
    w = np.where(on, w, rng.random((N, 8, 1, NC)) < 0.5)
    wa = rng.random((N, 8, E)) < 0.5; x = rng.random((N, 8, E)) < 0.75; x[..., 0] = True; x[..., -1] = True
    wb = wa ^ x
    c = np.argsort(rng.random((N, N, 8, B)), axis=-1) < cross[..., None]
    b = rng.random((N, N, 8, B)) < 0.5
    for q in range(N):
        for r in range(q + 1, N): b[r, q] = b[q, r] ^ c[q, r]
    tab = rng.integers(0, 12, (N, 16, 256 * KN)); tab[rng.random(tab.shape) < 0.2] = -1
    return {"lv": lv, "ch": f(rng, N, 128, NV), "cor": tables8(pick(rng, s, w.reshape(N, 8, 8 * NC), h)), "kd": rng.integers(0, KN, (N, 8, NC)).astype(np.int32),
            "ce": rng.integers(0, E + N * B, (N, 8, 12 * NC)).astype(np.int32), "ea": tables8(pick(rng, s, wa, h)), "eb": tables8(pick(rng, s, wb, h)),
            "bl": tables8(pick(rng, s, b.transpose(0, 2, 1, 3).reshape(N, 8, N * B), h)), "tab": tab.astype(np.int32)}
def sizes(rng):
    act = rng.integers(A >> 1, A + 1, (N, 8)); act[rng.integers(0, N), rng.integers(0, 8)] = A
    cross = rng.integers(CX >> 1, CX + 1, (N, N, 8)); q, r = np.sort(rng.choice(N, 2, replace=False)); cross[q, r, rng.integers(0, 8)] = CX
    return act, cross
def setup_inputs(rng):
    return make(rng, *sizes(rng))
def setup_inputs_full(rng):
    return make(rng, np.full((N, 8), A), np.full((N, N, 8), CX))
def setup_inputs_few(rng):
    act = rng.choice(np.array([0, 1, A >> 2]), (N, 8)); act[np.arange(N), rng.integers(0, 8, N)] = A >> 2
    return make(rng, act, rng.choice(np.array([0, 1, CX]), (N, N, 8)))
def setup_inputs_zeros(rng):
    d = make(rng, *sizes(rng), zero=0.5); tab = d["tab"]; w = rng.integers(0, 6, (N, 1, 256 * KN)); e = rng.integers(0, 12, w.shape).astype(np.int32)
    tab = np.where(w == 0, -1, np.where(w == 1, e, tab)); tab = np.where((w == 2) & (np.arange(16)[:, None] < 15), -1, np.where(w == 2, e, tab))
    d["tab"] = tab.astype(np.int32); return d
def setup_inputs_alike(rng):
    d = make(rng, *sizes(rng), h=True); p = rng.integers(0, E + N * B, (N, 8, 8)); p[..., 0] = 0; p[..., 1] = E + N * B - 1
    d["ce"] = np.take_along_axis(p, rng.integers(0, 8, (N, 8, 12 * NC)), -1).astype(np.int32)
    d["kd"] = np.repeat(rng.integers(0, KN, (N, 8, 1)), NC, axis=-1).astype(np.int32); return d
def setup_inputs_spread(rng):
    d = setup_inputs(rng); d["ch"] = wide(rng, N, 128, NV)
    d["lv"] = (d["lv"].astype(np.float32) * np.exp2(rng.integers(-6, 7, d["lv"].shape))).astype(BF); return d
def check_inputs(d):
    bad = [a for a, lo, hi in (("cor", 0, NV - 1), ("kd", 0, KN - 1), ("ce", 0, E + N * B - 1), ("ea", 0, NV - 1), ("eb", 0, NV - 1), ("bl", 0, NV - 1), ("tab", -1, 11)) if d[a].min() < lo or d[a].max() > hi]
    bad += [a for a in ("lv", "ch") if not np.isfinite(d[a].astype(np.float32)).all()]
    if bad: return bad
    s = d["lv"].astype(np.float32) < 0; c = cases(s, d["cor"])
    if np.sum((c > 0) & (c < 255), axis=-1).max() > A: bad.append("active cells")
    if np.sum(crossings(s, d["bl"]), axis=-1).max() > CX: bad.append("crossing border edges")
    return bad
def reference(lv, ch, cor, kd, ce, ea, eb, bl, tab):
    y = np.zeros((N, 128, 16 * A), np.float32); zero = np.float32(0)
    s = lv.astype(np.float32) < 0; c = ch.astype(np.float32).reshape(N, 8, 16, NV)
    case = cases(s, cor); cross = crossings(s, bl); la, lb, lx = lists8(ea), lists8(eb), lists8(bl).reshape(N, 8, N, B)
    for r in range(N):
        for g in range(8):
            v = np.zeros((16, E + N * B), np.float32); i, j = la[r, g], lb[r, g]
            v[:, :E] = np.where(s[r, g][i] != s[r, g][j], c[r, g][:, i] + c[r, g][:, j], zero)
            for q in range(N):
                v[:, E + q * B:E + (q + 1) * B] = np.where(cross[r, q, g], c[r, g][:, lx[r, g, q]] + c[q, g][:, lx[q, g, r]], zero)
            m = np.flatnonzero((case[r, g] > 0) & (case[r, g] < 255))
            e = tab[r][:, 256 * kd[r, g, m] + case[r, g, m]].T
            n = ce[r, g][12 * m[:, None] + np.maximum(e, 0)].reshape(-1)
            y[r, 16 * g:16 * g + 16, :16 * len(m)] = np.where(e.reshape(-1) >= 0, v[:, n], zero)
    return {"y": y}

@@ -1,0 +1,364 @@
+from concourse.bass import DstId, RemoteDMATransfer
+from concourse.mybir import AluOpType, ActivationFunctionType
+
+F32, BF, I32, U16 = "float32", "bfloat16", "int32", "uint16"
+NV, NC, NE, NB = 3072, 1024, 2048, 128
+PADC = 16
+ZC = NV + PADC
+BW = NB + 8
+ZU = PADC + 8 * BW
+DUMP = 1664
+CHUNKS = [16, 16, 40, 40, 40, 40, 24, 24, 8, 8]
+
+SBUF = {
+    BF: dict(lvs=[384], fl=[384], inw=[NV], chw=[NV + 2 * PADC], gcor=[8 * NC], gedg=[2 * NE], gb=[1024], xs=[8, BW],
+             xr=[8, BW], cb=[8, 16, 8], kdb=[128], tabb=[512], tabw=[4096], ca=[NE], sb=[256], uu=[128], ones=[144],
+             bs=[8, 128], ks=[8, 128], zz=[3, 144], zd=[36, 8], sel=[8], wk=[8, 8], idb=[128], bd0=[128], bd=[128],
+             lt=[128], ut=[128], rb=[72]),
+    F32: dict(us=[ZU + PADC], pf=[1], j0=[64], jc=[64], dh=[8, 16, 8], vt=[NV + 16], tb=[64], tb2=[64], te=[256],
+              pay=[NC], sw=[DUMP], posf=[256], posc=[256], ww=[4096], yy=[4096], idf=[128], cc=[64], wf=[64]),
+    I32: dict(bl32=[64], cor32=[512], eab32=[256], pi=[1], pr=[1], d32=[64, 12], kd32=[128], tab32=[512]),
+    U16: dict(bl16=[64], blc=[64], cor16=[512], eab16=[256], b16=[64], i16=[256], e16=[256], ti16=[16], pos16=[256],
+              off16=[64]),
+}
+SCRATCH = {k: ("sbuf", [128] + s, d) for d, bufs in SBUF.items() for k, s in bufs.items()}
+SCRATCH.update({"p%d" % b: ("psum", [128, 512], F32) for b in range(8)})
+
+SEMAPHORES = ["cv", "cs", "cp", "cg", "dlv", "dbl", "dcor", "deab", "dkd", "dce", "dch", "dtab", "drep",
+              "arr", "left", "dx", "dr", "dy"]
+
+
+def rank_program(g, core, T, topo):
+    rank = T.rank_of(core)
+    if rank is None:
+        return
+    A, AF = AluOpType, ActivationFunctionType
+    n = len(T.cores)
+
+    Q = {"v": g.vector, "s": g.scalar, "p": g.tensor, "g": g, "y": g.sync}
+    total = {}
+    known = {q: {} for q in Q}
+    writer, readers, bank = {}, {}, {}
+
+    def need(q, tok):
+        sem, cnt, seen = tok
+        if known[q].get(sem, 0) >= cnt:
+            return
+        Q[q].wait_ge(T.sem[sem], cnt)
+        known[q][sem] = cnt
+        for s, c in seen.items():
+            if known[q].get(s, 0) < c:
+                known[q][s] = c
+
+    def order(q, r, w, b):
+        toks = [writer[k] for k in r if k in writer]
+        for k in w:
+            toks += readers.get(k, []) + ([writer[k]] if k in writer else [])
+        for k in b:
+            toks += [t for o, t in bank.get(k, {}).items() if o != q]
+        best = {}
+        for t in toks:
+            if t[0] not in best or best[t[0]][1] < t[1]:
+                best[t[0]] = t
+        for t in sorted(best.values(), key=lambda t: -len(t[2])):
+            need(q, t)
+
+    def note(q, sem, inc, r, w, b):
+        total[sem] = total.get(sem, 0) + inc
+        tok = (sem, total[sem], dict(known[q]))
+        for k in r:
+            readers.setdefault(k, []).append(tok)
+        for k in w:
+            writer[k] = tok
+            readers[k] = []
+        for k in b:
+            bank.setdefault(k, {})[q] = tok
+
+    def op(q, fn, r=(), w=(), b=()):
+        order(q, r, w, b)
+        fn().then_inc(T.sem["c" + q], 1)
+        note(q, "c" + q, 1, r, w, b)
+
+    def dma(q, sem, out, in_, r=(), w=(), **kw):
+        order(q, r, w, ())
+        Q[q].dma_start(out, in_, **kw).then_inc(T.sem[sem], 16)
+        note(q, sem, 16, r, w, ())
+
+    V, S = g.vector, g.scalar
+    P = [T["p%d" % i] for i in range(8)]
+
+    def mm(b, out, lhsT, rhs, start, stop, r):
+        op("p", lambda: g.tensor.matmul(out, lhsT, rhs, start, stop), r=r, b=[b])
+
+    def ts(out, in0, s1, s2, o0, o1, r, w, b=()):
+        if o1 is None:
+            op("v", lambda: V.tensor_scalar(out, in0, s1, None, o0), r, w, b)
+        else:
+            op("v", lambda: V.tensor_scalar(out, in0, s1, s2, o0, o1), r, w, b)
+
+    def tt(out, in0, in1, o, r, w, b=()):
+        op("v", lambda: V.tensor_tensor(out, in0, in1, o), r, w, b)
+
+    def cp(q, out, in_, r, w, b=()):
+        if q == "v":
+            op("v", lambda: V.tensor_copy(out, in_), r, w, b)
+        else:
+            op("s", lambda: S.activation(out, in_, AF.Copy), r, w, b)
+
+    def scaled(out, in_, f, r, w):
+        op("s", lambda: S.activation(out, in_, AF.Copy, scale=f), r, w)
+
+    def fill(ap, val, w):
+        op("v", lambda: V.memset(ap, val), w=w)
+
+    def sel(out, in_, pat, cmp, fl, base, cm, r, w):
+        op("g", lambda: g.affine_select(out, in_, pat, cmp, fl, base, cm), r, w)
+
+    def iota(out, pat, base, cm, w):
+        op("g", lambda: g.iota(out, pat, base, cm, allow_small_or_imprecise_dtypes=True), w=w)
+
+    peers = [q for q in range(n) if q != rank]
+    spans = [(a, b) for a, b in ((0, rank), (rank + 1, n)) if b > a]
+
+    dma("y", "dlv", T.lvs[0:64, :], T.lv[:, :], w=["lvs"])
+    dma("s", "dbl", T.bl32[:, :], T.bl[:, :], w=["bl32"])
+    dma("s", "dcor", T.cor32[:, :], T.cor[:, :], w=["cor32"])
+    dma("s", "dkd", T.kd32[0:64, :], T.kd[:, :], w=["kd32"])
+    dma("y", "dch", T.chw[:, PADC:ZC], T.ch[:, :], w=["ch"])
+    dma("y", "dtab", T.tab32[:, :], T.tab[:, :], w=["tab32"])
+    for k in range(8):
+        dma("y", "dce", T.d32[:, 8 * k:8 * k + 8, :], T.ce[k, :], w=["d32"] if k == 7 else [])
+    dma("y", "deab", T.eab32[:, 0:128], T.ea[:, :])
+    dma("y", "deab", T.eab32[:, 128:256], T.eb[:, :], w=["eab32"])
+
+    iota(T.uu[0:64, :], [[-8, 8], [0, 16]], 0, 1, ["uu"])
+    fill(T.ones[:, :], 1.0, ["ones"])
+    fill(T.zz[:, :, :], 0.0, ["zz"])
+    for s in range(8):
+        ts(T.bs[0:64, s, :], T.uu[0:64, :], float(s), None, A.is_equal, None, ["uu"], ["bs%d" % s])
+    sel(T.sel[:, :], T.ones[:, 0:8], [[-16, 8]], A.is_equal, 0.0, 0, 1, ["ones"], ["sel"])
+    op("g", lambda: g.iota(T.pi[:, :], [[0, 1]], 0, 1), w=["pi"])
+    iota(T.j0[:, :], [[BW, 8], [16, 8]], PADC - NV, 0, ["j0"])
+    for ap, w, k in ((T.gb[:, NB * rank:NB * rank + NB], NB, "gbo"), (T.xs[:, rank, 0:NB], NB, "xo"), (T.xr[:, rank, :], BW, "ro"),
+                     (T.chw[:, 0:PADC], PADC, "chz0"), (T.chw[:, ZC:ZC + PADC], PADC, "chz1"), (T.vt[:, NV:NV + 16], 16, "vz"),
+                     (T.vt[:, NE + NB * rank:NE + NB * rank + NB], NB, "vo"), (T.us[:, 0:PADC], PADC, "usz0"),
+                     (T.us[:, ZU:ZU + PADC], PADC, "usz1"), (T.rb[:, 0:1], 1, "rb0"),
+                     (T.zd[:, 0:18, :], 144, "zd0"), (T.zd[:, 18:36, :], 144, "zd1")):
+        scaled(ap, T.ones[:, 0:w], 0.0, ["ones"], [k])
+    for k in range(8):
+        scaled(T.wk[:, k, :], T.sel[:, :], float(2 ** k), ["sel"], ["wk%d" % k])
+    scaled(T.dh[:, :, 0, :], T.ones[:, 0:64], float(NV), ["ones"], ["dh0"])
+    sel(T.idb[:, :], T.ones[:, 0:128], [[-1, 128]], A.is_equal, 0.0, 0, 1, ["ones"], ["idb"])
+    sel(T.idf[:, :], T.ones[:, 0:128], [[-1, 128]], A.is_equal, 0.0, 0, 1, ["ones"], ["idf"])
+    sel(T.zz[:, 0, 15:143:16], T.zz[:, 0, 14:142:16], [[-16, 8]], A.not_equal, float(NV), 0, 1, ["zz"], ["z1"])
+    sel(T.ks[0:64, :, :], T.bs[0:64, :, :], [[0, 64], [1, 16]], A.is_equal, 0.0, -13, 0,
+        ["bs%d" % s for s in range(8)], ["ks"])
+    sel(T.bd0[:, :], T.ones[:, 0:128], [[-16, 8], [0, 16]], A.is_ge, 0.0, 0, 1, ["ones"], ["bd0"])
+    sel(T.bd[:, :], T.bd0[:, :], [[16, 8], [0, 16]], A.is_ge, 0.0, 15, -1, ["bd0"], ["bd"])
+    sel(T.lt[:, :], T.bd[:, :], [[1, 128]], A.is_gt, 0.0, 0, -1, ["bd"], ["lt"])
+    sel(T.ut[:, :], T.bd[:, :], [[-1, 128]], A.is_ge, 0.0, 0, 1, ["bd"], ["ut"])
+    iota(T.cc[:, :], [[16, 64]], 256, 1, ["cc"])
+    sel(T.zz[:, 2, 0:8], T.zz[:, 2, 8:16], [[-16, 8]], A.not_equal, 256.0, -13, 1, ["zz"], ["z2a"])
+    sel(T.zz[:, 1, 15:143:16], T.zz[:, 2, 0:8], [[-16, 8]], A.not_equal, 1.0, -14, 1, ["z2a"], ["z2"])
+    ts(T.pr[:, :], T.pi[:, :], 15, None, A.bitwise_and, None, ["pi"], ["pr"])
+    fill(T.cb[:, :, :, :], 0.0, ["cb"])
+    cp("v", T.pf[:, :], T.pr[:, :], ["pr"], ["pf"])
+
+    ts(T.fl[0:64, :], T.lvs[0:64, :], 0.0, None, A.is_lt, None, ["lvs"], ["fl"])
+    for s in range(8):
+        c = 384 * s
+        while c < 384 * s + 384:
+            e = min(384 * s + 384, (c // 512 + 1) * 512)
+            mm(c // 512, P[c // 512][:, c % 512:c % 512 + e - c], T.bs[0:64, s, :], T.fl[0:64, c - 384 * s:e - 384 * s],
+               True, True, ["bs%d" % s, "fl"])
+            c = e
+    cp("v", T.bl16[:, :], T.bl32[:, :], ["bl32"], ["bl16"])
+    ts(T.blc[:, :], T.bl32[:, :], float(PADC), None, A.add, None, ["bl32"], ["blc"])
+    fill(T.dh[:, :, 13:16, :], 0.0, ["dh1"])
+    ts(T.jc[:, :], T.j0[:, :], T.pf[:, :], None, A.add, None, ["j0", "pf"], ["jc"])
+    cp("v", T.cor16[:, :], T.cor32[:, :], ["cor32"], ["cor16"])
+    for b in range(6):
+        cp("s" if b < 4 else "v", T.inw[:, 512 * b:512 * b + 512], P[b][:, :], [], ["in%d" % b], [b])
+    IN = ["in%d" % b for b in range(6)]
+    CH = ["ch", "chz0", "chz1"]
+
+    def corner(q, k, h=None):
+        a, b = (0, 64) if h is None else (32 * h, 32 * h + 32)
+        cp(q, T.gcor[:, NC * k + 16 * a:NC * k + 16 * b], T.inw[:, :].indirect(T.cor16[:, 64 * k + a:64 * k + b]),
+           IN + ["cor16"], ["gc%d_%d" % (k, i) for i in range(a // 32, b // 32)])
+
+    done = []
+
+    def case_mm(k):
+        done.append(k)
+        for c in range(8):
+            mm(2, P[2][:, c:64:8], T.gcor[:, NC * k + c:NC * k + NC:8], T.wk[:, k, :], False, len(done) == 8 and c == 7,
+               ["gc%d_0" % k, "gc%d_1" % k, "wk%d" % k])
+
+    def edge_in(q, end, a, b):
+        cp(q, T.gedg[:, NE * end + 512 * a:NE * end + 512 * b],
+           T.inw[:, :].indirect(T.eab16[:, 128 * end + 32 * a:128 * end + 32 * b]),
+           IN + ["eab16"], ["ge%d_%d" % (end, i) for i in range(a, b)])
+
+    def edge_mm(h, end):
+        b = (3, 6)[h]
+        o = NE * end + 1024 * h
+        for c in range(16):
+            mm(b, P[b][:, 0:64], T.zz[:, 0, 15 - c:143 - c], T.gedg[:, o + c:o + 1024:16], end == h ^ 1 and c == 0,
+               end == h and c == 15, ["z1", "ge%d_%d" % (end, 2 * h), "ge%d_%d" % (end, 2 * h + 1)])
+
+    def edge_sum(h):
+        b = (3, 6)[h]
+        for end in range(2):
+            tt(T.te[:, 128 * h + 64 * end:128 * h + 64 * end + 64], P[b][:, 0:64],
+               T.eab32[:, 128 * end + 64 * h:128 * end + 64 * h + 64], A.add, ["eab32"], ["te%d_%d" % (h, end)], [b])
+
+    def edge_idx(h):
+        ts(T.i16[:, 128 * h:128 * h + 128], T.te[:, 128 * h:128 * h + 128], float(PADC - NV), float(ZC), A.add, A.min,
+           ["te%d_0" % h, "te%d_1" % h], ["i16_%d" % h])
+
+    def end_a(i):
+        o = 128 * (i // 2) + 32 * (i % 2)
+        cp("s", T.ca[:, 512 * i:512 * i + 512], T.chw[:, :].indirect(T.i16[:, o:o + 32]), CH + ["i16_%d" % (i // 2)], ["ca%d" % i])
+
+    def end_b(i):
+        o = 128 * (i // 2) + 32 * (i % 2) + 64
+        tt(T.vt[:, 512 * i:512 * i + 512], T.chw[:, :].indirect(T.i16[:, o:o + 32]), T.ca[:, 512 * i:512 * i + 512], A.add,
+           CH + ["i16_%d" % (i // 2), "ca%d" % i], ["vt%d" % i])
+
+    def scatter(a, b):
+        cp("v", T.sw[:, :].indirect(T.off16[:, a:b]), T.pay[:, 16 * a:16 * b], ["off16", "pay0", "pay1"], ["sw"])
+
+    for a, b in spans:
+        cp("s", T.gb[:, NB * a:NB * b], T.inw[:, :].indirect(T.bl16[:, 8 * a:8 * b]), IN + ["bl16"], ["gb%d" % a])
+    corner("v", 0)
+    for c in range(16):
+        mm(6, P[6][:, 0:64], T.zz[:, 0, 15 - c:143 - c], T.gb[:, c:1024:16], c == 0, c == 15,
+           ["z1", "gbo"] + ["gb%d" % a for a, b in spans])
+    for q in peers:
+        cp("s", T.xs[:, q, 0:NB], T.chw[:, :].indirect(T.blc[:, 8 * q:8 * q + 8]), CH + ["blc"], ["x%d" % q])
+    cp("s", T.xs[:, :, NB:BW], P[6][:, 0:64], [], ["fs"], [6])
+    xs = ["fs", "xo"] + ["x%d" % q for q in peers]
+    far = [q for q in peers if topo.die(T.cores[q]) != topo.die(core)]
+    near = [q for q in peers if q not in far]
+    order("g", xs, (), ())
+    tr = []
+    for q in peers:
+        en = topo.engines(core, T.cores[q])
+        i = 4 * far.index(q) if q in far else 4 * near.index(q) + 1
+        rid, pid, _ = topo.addr(T.cores[q])
+        tr.append(RemoteDMATransfer(dst_ids=[DstId(rid=rid, pnc=pid)], dma_engine_mask=(1 << en[i]) | (1 << en[i + 2]),
+                                    remote_sem=T.sem.arr, src=T.xs[:, q, :], dst=T.xr[:, rank, :]))
+    g.remote_dma_fused(tr, local_sem=T.sem.left)
+    for k in ("arr", "left"):
+        total[k] = 2 * len(peers)
+        writer[k] = (k, total[k], {})
+    dma("g", "dx", T.us[:, PADC:ZU], T.xs[:, :, :], xs, ["us"])
+    iota(T.sw[:, 0:256], [[0, 256]], NV, 0, ["sw"])
+    m0 = 0
+    for i, c in enumerate(CHUNKS):
+        if i % 2 == 0:
+            iota(T.posc[:, m0:m0 + 2 * c], [[0, 2], [16, c]], 1, 0, ["posc%d" % i])
+        m0 += c
+    dma("g", "dr", T.us[:, PADC:ZU], T.xr[:, :, :], ["arr", "ro"], ["us"], accum_op=A.add)
+
+    mm(2, P[2][:, 0:64], T.cb[:, 0, :, :], T.inw[:, 0:64], True, False, ["cb", "in0"])
+    for b in range(2):
+        mm(b, P[b][:, :], T.cb[:, 0, :, :], T.inw[:, 0:512], True, False, ["cb", "in0"])
+    case_mm(0)
+    cp("v", T.kdb[0:64, :], T.kd32[0:64, :], ["kd32"], ["kdb"])
+    for s in range(8):
+        mm(s // 4, P[s // 4][:, 128 * (s % 4):128 * (s % 4) + 128], T.ks[0:64, s, :], T.kdb[0:64, :], False, False, ["ks", "kdb"])
+    corner("s", 7)
+    corner("v", 1)
+    case_mm(1)
+    cp("v", T.tabb[:, :], T.tab32[:, :], ["tab32"], ["tabb"])
+    for k in range(8):
+        dma("y", "drep", T.tabw[16 * k:16 * k + 16, :], T.tabb[:, :], ["tabb"], ["tabw"] if k == 7 else [])
+    corner("v", 2)
+    case_mm(7)
+    case_mm(2)
+    for c in range(8):
+        cp("v", T.dh[:, :, 1:13, c], T.d32[:, c:64:8, :], ["d32"], ["dh_%d" % c])
+    corner("s", 6)
+    case_mm(6)
+    for b in range(2):
+        for c in range(8):
+            mm(b, P[b][:, c:512:8], T.dh[:, :, :, c], T.idf[:, 64 * b:64 * b + 64], False, False,
+               ["dh0", "dh1", "dh_%d" % c, "idf"])
+    corner("v", 3)
+    corner("s", 5)
+    case_mm(3)
+    case_mm(5)
+    cp("v", T.eab16[:, :], T.eab32[:, :], ["eab32"], ["eab16"])
+    corner("s", 4, 0)
+    corner("v", 4, 1)
+    case_mm(4)
+    tt(T.tb[:, :], T.xs[:, :, NB:BW], T.jc[:, :], A.add, ["fs", "jc"], ["tb"])
+    edge_in("s", 1, 0, 1)
+
+    ts(T.zd[:, 1:17:2, :], P[2][:, 0:64], 1.0, None, A.is_lt, None, ["zd0"], ["d0"], [2])
+    ts(T.zd[:, 19:35:2, :], P[2][:, 0:64], 255.0, None, A.is_ge, None, ["zd1"], ["d1"], [2])
+    cp("v", T.cb[:, :, 14, :], P[2][:, 0:64], [], ["cb"], [2])
+    for i, (d, k) in enumerate(((1, "d0"), (19, "d1"))):
+        for h in range(2):
+            mm(4, P[4][:, 0:64], T.zd[:, d - h:d - h + 16, :], T.idb[:, h:128:2], i + h == 0, i + h == 2, [k, "idb"])
+    for b in range(2):
+        for c in range(8):
+            mm(b, P[b][:, c:512:8], T.cb[:, :, :, c], T.idb[:, 64 * b:64 * b + 64], False, c == 7, ["cb", "idb"])
+    edge_in("s", 0, 0, 1)
+    op("v", lambda: V.tensor_tensor_scan(T.rb[:, 1:65], T.ones[:, 0:64], P[4][:, 0:64], 0.0, A.add, A.subtract),
+       ["ones"], ["rb"], [4])
+    tt(T.wf[:, :], P[4][:, 0:64], T.cc[:, :], A.mult, ["cc"], ["wf"], [4])
+    mm(5, P[5][:, 0:64], T.lt[:, :], T.rb[:, 1:65], True, False, ["lt", "rb"])
+    mm(5, P[5][:, 0:64], T.ut[:, :], T.rb[:, 0:64], False, False, ["ut", "rb", "rb0"])
+    mm(5, P[5][:, 0:64], T.idf[:, :], T.wf[:, :], False, True, ["idf", "wf"])
+    for b in range(2):
+        cp("s", T.pay[:, 512 * b:512 * b + 512], P[b][:, :], [], ["pay%d" % b], [b])
+    edge_in("v", 1, 1, 2)
+    cp("v", T.off16[:, :], P[5][:, 0:64], [], ["off16"], [5])
+    edge_mm(0, 1)
+    edge_in("s", 0, 1, 2)
+    edge_mm(0, 0)
+    edge_in("s", 0, 2, 4)
+    edge_mm(1, 0)
+    edge_in("s", 1, 2, 4)
+    edge_mm(1, 1)
+    scatter(0, 48)
+    edge_sum(0)
+    tt(T.tb2[:, :], T.xr[:, :, NB:BW], T.tb[:, :], A.add, ["tb", "arr", "ro"], ["tb2"])
+    edge_idx(0)
+    ts(T.b16[:, :], T.tb2[:, :], 0.0, float(ZU), A.max, A.min, ["tb2"], ["b16"])
+    scatter(48, 64)
+    edge_sum(1)
+    cp("v", T.e16[:, :], T.sw[:, 0:256], ["sw"], ["e16"])
+    edge_idx(1)
+    end_a(0)
+    cp("s", T.sb[:, :], T.sw[:, 0:256], ["sw"], ["sb"])
+    for t in range(16):
+        mm(7, P[7][:, 0:16], T.zz[:, 1, 15 - t:143 - t], T.sb[:, t:256:16], t == 0, t == 15, ["z2", "sb"])
+    end_a(1)
+    end_b(0)
+    ts(T.ti16[:, :], P[7][:, 0:16], 4095.0, None, A.min, None, [], ["ti16"], [7])
+    end_b(1)
+    tt(T.posf[:, :], T.tabw[:, :].indirect(T.ti16[:, :]), T.posc[:, :], A.add,
+       ["tabw", "ti16"] + ["posc%d" % i for i in range(0, len(CHUNKS), 2)], ["posf"])
+    end_a(2)
+    end_a(3)
+    for a, b in spans:
+        cp("s", T.vt[:, NE + NB * a:NE + NB * b], T.us[:, :].indirect(T.b16[:, 8 * a:8 * b]),
+           ["us", "usz0", "usz1", "b16"], ["vb%d" % a])
+    end_b(2)
+    cp("v", T.pos16[:, :], T.posf[:, :], ["posf"], ["pos16"])
+    end_b(3)
+
+    VT = ["vt0", "vt1", "vt2", "vt3", "vo", "vz"] + ["vb%d" % a for a, b in spans]
+    m0 = 0
+    for i, c in enumerate(CHUNKS):
+        q, m, w = "vs"[i % 2], slice(m0, m0 + c), slice(16 * m0, 16 * (m0 + c))
+        cp(q, T.ww[:, w], T.vt[:, :].indirect(T.e16[:, m]), VT + ["e16"], ["w%d" % i])
+        cp(q, T.yy[:, w], T.ww[:, w].indirect(T.pos16[:, m]), ["w%d" % i, "pos16"], ["y%d" % i])
+        dma("y", "dy", T.y[:, w], T.yy[:, w], ["y%d" % i], ["out%d" % i])
+        m0 += c
+    for sem, cnt in total.items():
+        need("y", (sem, cnt, {}))

@@ -9,6 +9,10 @@ BW = NB + 8
 ZU = PADC + 8 * BW
 DUMP = 1664
 CHUNKS = [16, 16, 40, 40, 40, 40, 24, 24, 8, 8]
+PLAN = ("v K w01 w21 w40 w11 w31 w50 D z F c110 c210 c200 X R c410 c711 c611 x r1 C c401 c000 u r0 m2 G c601 P c511 m4 c501 "
+        "S c010 Z t c300 m0 c701 c310 e001 m6 m5 c100 e100 m3 m1 m7 M A e110 e031 N p00 e011 e021 e131 T f00 f01 p11 o s0 g0 "
+        "s1 h0 e121 f10 f11 s3 U s2 a0 a1 g1 l h1 k1 b0 b1 i a2 a3 b2 j B b3 J "
+        "W30 W10 y10 W21 W01 W41 y30 W90 W50 y21 y41 y01 W61 y50 y61 W70 y91 W81 y70 y81")
 
 SBUF = {
     BF: dict(lvs=[384], fl=[384], inw=[NV], chw=[NV + 2 * PADC], gcor=[8 * NC], gedg=[2 * NE], gb=[1024], xs=[8, BW],
@@ -51,7 +55,7 @@ def rank_program(g, core, T, topo):
                 known[q][s] = c
 
     def order(q, r, w, b):
-        toks = [writer[k] for k in r if k in writer]
+        toks = [writer[k] for k in r]
         for k in w:
             toks += readers.get(k, []) + ([writer[k]] if k in writer else [])
         for k in b:
@@ -84,7 +88,7 @@ def rank_program(g, core, T, topo):
         Q[q].dma_start(out, in_, **kw).then_inc(T.sem[sem], 16)
         note(q, sem, 16, r, w, ())
 
-    V, S = g.vector, g.scalar
+    V, S, QS = g.vector, g.scalar, "vs"
     P = [T["p%d" % i] for i in range(8)]
 
     def mm(b, out, lhsT, rhs, start, stop, r):
@@ -114,6 +118,9 @@ def rank_program(g, core, T, topo):
     def sel(out, in_, pat, cmp, fl, base, cm, r, w):
         op("g", lambda: g.affine_select(out, in_, pat, cmp, fl, base, cm), r, w)
 
+    def convert(out, in_, k, r, w):
+        sel(out, in_, [[0, k]], A.is_ge, 0.0, 0, 0, r, w)
+
     def iota(out, pat, base, cm, w):
         op("g", lambda: g.iota(out, pat, base, cm, allow_small_or_imprecise_dtypes=True), w=w)
 
@@ -124,12 +131,12 @@ def rank_program(g, core, T, topo):
     dma("s", "dbl", T.bl32[:, :], T.bl[:, :], w=["bl32"])
     dma("s", "dcor", T.cor32[:, :], T.cor[:, :], w=["cor32"])
     dma("s", "dkd", T.kd32[0:64, :], T.kd[:, :], w=["kd32"])
-    dma("y", "dch", T.chw[:, PADC:ZC], T.ch[:, :], w=["ch"])
-    dma("y", "dtab", T.tab32[:, :], T.tab[:, :], w=["tab32"])
     for k in range(8):
         dma("y", "dce", T.d32[:, 8 * k:8 * k + 8, :], T.ce[k, :], w=["d32"] if k == 7 else [])
+    dma("y", "dch", T.chw[:, PADC:ZC], T.ch[:, :], w=["ch"])
     dma("y", "deab", T.eab32[:, 0:128], T.ea[:, :])
     dma("y", "deab", T.eab32[:, 128:256], T.eb[:, :], w=["eab32"])
+    dma("y", "dtab", T.tab32[:, :], T.tab[:, :], w=["tab32"])
 
     iota(T.uu[0:64, :], [[-8, 8], [0, 16]], 0, 1, ["uu"])
     fill(T.ones[:, :], 1.0, ["ones"])
@@ -151,15 +158,6 @@ def rank_program(g, core, T, topo):
     sel(T.idb[:, :], T.ones[:, 0:128], [[-1, 128]], A.is_equal, 0.0, 0, 1, ["ones"], ["idb"])
     sel(T.idf[:, :], T.ones[:, 0:128], [[-1, 128]], A.is_equal, 0.0, 0, 1, ["ones"], ["idf"])
     sel(T.zz[:, 0, 15:143:16], T.zz[:, 0, 14:142:16], [[-16, 8]], A.not_equal, float(NV), 0, 1, ["zz"], ["z1"])
-    sel(T.ks[0:64, :, :], T.bs[0:64, :, :], [[0, 64], [1, 16]], A.is_equal, 0.0, -13, 0,
-        ["bs%d" % s for s in range(8)], ["ks"])
-    sel(T.bd0[:, :], T.ones[:, 0:128], [[-16, 8], [0, 16]], A.is_ge, 0.0, 0, 1, ["ones"], ["bd0"])
-    sel(T.bd[:, :], T.bd0[:, :], [[16, 8], [0, 16]], A.is_ge, 0.0, 15, -1, ["bd0"], ["bd"])
-    sel(T.lt[:, :], T.bd[:, :], [[1, 128]], A.is_gt, 0.0, 0, -1, ["bd"], ["lt"])
-    sel(T.ut[:, :], T.bd[:, :], [[-1, 128]], A.is_ge, 0.0, 0, 1, ["bd"], ["ut"])
-    iota(T.cc[:, :], [[16, 64]], 256, 1, ["cc"])
-    sel(T.zz[:, 2, 0:8], T.zz[:, 2, 8:16], [[-16, 8]], A.not_equal, 256.0, -13, 1, ["zz"], ["z2a"])
-    sel(T.zz[:, 1, 15:143:16], T.zz[:, 2, 0:8], [[-16, 8]], A.not_equal, 1.0, -14, 1, ["z2a"], ["z2"])
     ts(T.pr[:, :], T.pi[:, :], 15, None, A.bitwise_and, None, ["pi"], ["pr"])
     fill(T.cb[:, :, :, :], 0.0, ["cb"])
     cp("v", T.pf[:, :], T.pr[:, :], ["pr"], ["pf"])
@@ -176,36 +174,61 @@ def rank_program(g, core, T, topo):
     ts(T.blc[:, :], T.bl32[:, :], float(PADC), None, A.add, None, ["bl32"], ["blc"])
     fill(T.dh[:, :, 13:16, :], 0.0, ["dh1"])
     ts(T.jc[:, :], T.j0[:, :], T.pf[:, :], None, A.add, None, ["j0", "pf"], ["jc"])
-    cp("v", T.cor16[:, :], T.cor32[:, :], ["cor32"], ["cor16"])
-    for b in range(6):
-        cp("s" if b < 4 else "v", T.inw[:, 512 * b:512 * b + 512], P[b][:, :], [], ["in%d" % b], [b])
     IN = ["in%d" % b for b in range(6)]
     CH = ["ch", "chz0", "chz1"]
+    xs = ["fs", "xo"] + ["x%d" % q for q in peers]
+    VT = ["vt0", "vt1", "vt2", "vt3", "vo", "vz"] + ["vb%d" % a for a, b in spans]
+    at = [sum(CHUNKS[:i]) for i in range(len(CHUNKS) + 1)]
+    done, cases = [], []
 
-    def corner(q, k, h=None):
-        a, b = (0, 64) if h is None else (32 * h, 32 * h + 32)
-        cp(q, T.gcor[:, NC * k + 16 * a:NC * k + 16 * b], T.inw[:, :].indirect(T.cor16[:, 64 * k + a:64 * k + b]),
-           IN + ["cor16"], ["gc%d_%d" % (k, i) for i in range(a // 32, b // 32)])
+    def flags_out():
+        gbs = ["z1", "gbo"]
+        for q, lo, hi in (("v", 0, n // 2), ("s", n // 2, n)):
+            for a, b in spans:
+                a, b = max(a, lo), min(b, hi)
+                if b > a:
+                    cp(q, T.gb[:, NB * a:NB * b], T.inw[:, :].indirect(T.bl16[:, 8 * a:8 * b]), IN + ["bl16"], ["gb%d" % a])
+                    gbs.append("gb%d" % a)
+        for c in range(16):
+            mm(6, P[6][:, 0:64], T.zz[:, 0, 15 - c:143 - c], T.gb[:, c:1024:16], c == 0, c == 15, gbs)
 
-    done = []
+    def ends_out():
+        for q in peers:
+            cp("s", T.xs[:, q, 0:NB], T.chw[:, :].indirect(T.blc[:, 8 * q:8 * q + 8]), CH + ["blc"], ["x%d" % q])
+        cp("s", T.xs[:, :, NB:BW], P[6][:, 0:64], [], ["fs"], [6])
 
-    def case_mm(k):
-        done.append(k)
-        for c in range(8):
-            mm(2, P[2][:, c:64:8], T.gcor[:, NC * k + c:NC * k + NC:8], T.wk[:, k, :], False, len(done) == 8 and c == 7,
-               ["gc%d_0" % k, "gc%d_1" % k, "wk%d" % k])
+    def send():
+        far = [q for q in peers if topo.die(T.cores[q]) != topo.die(core)]
+        near = [q for q in peers if q not in far]
+        order("g", xs, (), ())
+        tr = []
+        for q in peers:
+            en = topo.engines(core, T.cores[q])
+            i = 4 * far.index(q) if q in far else 4 * near.index(q) + 1
+            rid, pid, _ = topo.addr(T.cores[q])
+            tr.append(RemoteDMATransfer(dst_ids=[DstId(rid=rid, pnc=pid)], dma_engine_mask=(1 << en[i]) | (1 << en[i + 2]),
+                                        remote_sem=T.sem.arr, src=T.xs[:, q, :], dst=T.xr[:, rank, :]))
+        g.remote_dma_fused(tr, local_sem=T.sem.left)
+        for k in ("arr", "left"):
+            total[k] = 2 * len(peers)
+            writer[k] = (k, total[k], {})
 
-    def edge_in(q, end, a, b):
-        cp(q, T.gedg[:, NE * end + 512 * a:NE * end + 512 * b],
-           T.inw[:, :].indirect(T.eab16[:, 128 * end + 32 * a:128 * end + 32 * b]),
-           IN + ["eab16"], ["ge%d_%d" % (end, i) for i in range(a, b)])
+    def border():
+        for a, b in spans:
+            cp("s", T.vt[:, NE + NB * a:NE + NB * b], T.us[:, :].indirect(T.b16[:, 8 * a:8 * b]),
+               ["us", "usz0", "usz1", "b16"], ["vb%d" % a])
+
+    def edge_in(end, i, q):
+        cp(QS[q], T.gedg[:, NE * end + 512 * i:NE * end + 512 * i + 512],
+           T.inw[:, :].indirect(T.eab16[:, 128 * end + 32 * i:128 * end + 32 * i + 32]), IN + ["eab16"], ["ge%d_%d" % (end, i)])
 
     def edge_mm(h, end):
         b = (3, 6)[h]
         o = NE * end + 1024 * h
         for c in range(16):
-            mm(b, P[b][:, 0:64], T.zz[:, 0, 15 - c:143 - c], T.gedg[:, o + c:o + 1024:16], end == h ^ 1 and c == 0,
-               end == h and c == 15, ["z1", "ge%d_%d" % (end, 2 * h), "ge%d_%d" % (end, 2 * h + 1)])
+            mm(b, P[b][:, 0:64], T.zz[:, 0, 15 - c:143 - c], T.gedg[:, o + c:o + 1024:16], h not in done and c == 0,
+               h in done and c == 15, ["z1", "ge%d_%d" % (end, 2 * h), "ge%d_%d" % (end, 2 * h + 1)])
+        done.append(h)
 
     def edge_sum(h):
         b = (3, 6)[h]
@@ -226,139 +249,116 @@ def rank_program(g, core, T, topo):
         tt(T.vt[:, 512 * i:512 * i + 512], T.chw[:, :].indirect(T.i16[:, o:o + 32]), T.ca[:, 512 * i:512 * i + 512], A.add,
            CH + ["i16_%d" % (i // 2), "ca%d" % i], ["vt%d" % i])
 
-    def scatter(a, b):
-        cp("v", T.sw[:, :].indirect(T.off16[:, a:b]), T.pay[:, 16 * a:16 * b], ["off16", "pay0", "pay1"], ["sw"])
+    def corner(k, h, q):
+        cp(QS[q], T.gcor[:, NC * k + 512 * h:NC * k + 512 * h + 512],
+           T.inw[:, :].indirect(T.cor16[:, 64 * k + 32 * h:64 * k + 32 * h + 32]), IN + ["cor16"], ["gc%d_%d" % (k, h)])
 
-    for a, b in spans:
-        cp("s", T.gb[:, NB * a:NB * b], T.inw[:, :].indirect(T.bl16[:, 8 * a:8 * b]), IN + ["bl16"], ["gb%d" % a])
-    corner("v", 0)
-    for c in range(16):
-        mm(6, P[6][:, 0:64], T.zz[:, 0, 15 - c:143 - c], T.gb[:, c:1024:16], c == 0, c == 15,
-           ["z1", "gbo"] + ["gb%d" % a for a, b in spans])
-    for q in peers:
-        cp("s", T.xs[:, q, 0:NB], T.chw[:, :].indirect(T.blc[:, 8 * q:8 * q + 8]), CH + ["blc"], ["x%d" % q])
-    cp("s", T.xs[:, :, NB:BW], P[6][:, 0:64], [], ["fs"], [6])
-    xs = ["fs", "xo"] + ["x%d" % q for q in peers]
-    far = [q for q in peers if topo.die(T.cores[q]) != topo.die(core)]
-    near = [q for q in peers if q not in far]
-    order("g", xs, (), ())
-    tr = []
-    for q in peers:
-        en = topo.engines(core, T.cores[q])
-        i = 4 * far.index(q) if q in far else 4 * near.index(q) + 1
-        rid, pid, _ = topo.addr(T.cores[q])
-        tr.append(RemoteDMATransfer(dst_ids=[DstId(rid=rid, pnc=pid)], dma_engine_mask=(1 << en[i]) | (1 << en[i + 2]),
-                                    remote_sem=T.sem.arr, src=T.xs[:, q, :], dst=T.xr[:, rank, :]))
-    g.remote_dma_fused(tr, local_sem=T.sem.left)
-    for k in ("arr", "left"):
-        total[k] = 2 * len(peers)
-        writer[k] = (k, total[k], {})
-    dma("g", "dx", T.us[:, PADC:ZU], T.xs[:, :, :], xs, ["us"])
-    iota(T.sw[:, 0:256], [[0, 256]], NV, 0, ["sw"])
-    m0 = 0
-    for i, c in enumerate(CHUNKS):
-        if i % 2 == 0:
-            iota(T.posc[:, m0:m0 + 2 * c], [[0, 2], [16, c]], 1, 0, ["posc%d" % i])
-        m0 += c
-    dma("g", "dr", T.us[:, PADC:ZU], T.xr[:, :, :], ["arr", "ro"], ["us"], accum_op=A.add)
+    def zero():
+        mm(2, P[2][:, 0:64], T.cb[:, 0, :, :], T.inw[:, 0:64], True, False, ["cb", "in0"])
+        for b in range(2):
+            mm(b, P[b][:, :], T.cb[:, 0, :, :], T.inw[:, 0:512], True, False, ["cb", "in0"])
 
-    mm(2, P[2][:, 0:64], T.cb[:, 0, :, :], T.inw[:, 0:64], True, False, ["cb", "in0"])
-    for b in range(2):
-        mm(b, P[b][:, :], T.cb[:, 0, :, :], T.inw[:, 0:512], True, False, ["cb", "in0"])
-    case_mm(0)
-    cp("v", T.kdb[0:64, :], T.kd32[0:64, :], ["kd32"], ["kdb"])
-    for s in range(8):
-        mm(s // 4, P[s // 4][:, 128 * (s % 4):128 * (s % 4) + 128], T.ks[0:64, s, :], T.kdb[0:64, :], False, False, ["ks", "kdb"])
-    corner("s", 7)
-    corner("v", 1)
-    case_mm(1)
-    cp("v", T.tabb[:, :], T.tab32[:, :], ["tab32"], ["tabb"])
-    for k in range(8):
-        dma("y", "drep", T.tabw[16 * k:16 * k + 16, :], T.tabb[:, :], ["tabb"], ["tabw"] if k == 7 else [])
-    corner("v", 2)
-    case_mm(7)
-    case_mm(2)
-    for c in range(8):
-        cp("v", T.dh[:, :, 1:13, c], T.d32[:, c:64:8, :], ["d32"], ["dh_%d" % c])
-    corner("s", 6)
-    case_mm(6)
-    for b in range(2):
+    def case_mm(k):
+        cases.append(k)
+        for c in range(8):
+            mm(2, P[2][:, c:64:8], T.gcor[:, NC * k + c:NC * k + NC:8], T.wk[:, k, :], False, len(cases) == 8 and c == 7,
+               ["gc%d_0" % k, "gc%d_1" % k, "wk%d" % k])
+
+    def kinds_in():
+        sel(T.ks[0:64, :, :], T.bs[0:64, :, :], [[0, 64], [1, 16]], A.is_equal, 0.0, -13, 0,
+            ["bs%d" % s for s in range(8)], ["ks"])
+        convert(T.kdb[0:64, :], T.kd32[0:64, :], 128, ["kd32"], ["kdb"])
+
+    def kinds_mm():
+        for s in range(8):
+            mm(s // 4, P[s // 4][:, 128 * (s % 4):128 * (s % 4) + 128], T.ks[0:64, s, :], T.kdb[0:64, :], False, False,
+               ["ks", "kdb"])
+
+    def cells_in():
+        for c in range(8):
+            convert(T.dh[:, :, 1:13, c], T.d32[:, c:64:8, :], 96, ["d32"], ["dh_%d" % c])
+
+    def rows(b):
         for c in range(8):
             mm(b, P[b][:, c:512:8], T.dh[:, :, :, c], T.idf[:, 64 * b:64 * b + 64], False, False,
                ["dh0", "dh1", "dh_%d" % c, "idf"])
-    corner("v", 3)
-    corner("s", 5)
-    case_mm(3)
-    case_mm(5)
-    cp("v", T.eab16[:, :], T.eab32[:, :], ["eab32"], ["eab16"])
-    corner("s", 4, 0)
-    corner("v", 4, 1)
-    case_mm(4)
-    tt(T.tb[:, :], T.xs[:, :, NB:BW], T.jc[:, :], A.add, ["fs", "jc"], ["tb"])
-    edge_in("s", 1, 0, 1)
 
-    ts(T.zd[:, 1:17:2, :], P[2][:, 0:64], 1.0, None, A.is_lt, None, ["zd0"], ["d0"], [2])
-    ts(T.zd[:, 19:35:2, :], P[2][:, 0:64], 255.0, None, A.is_ge, None, ["zd1"], ["d1"], [2])
-    cp("v", T.cb[:, :, 14, :], P[2][:, 0:64], [], ["cb"], [2])
-    for i, (d, k) in enumerate(((1, "d0"), (19, "d1"))):
-        for h in range(2):
-            mm(4, P[4][:, 0:64], T.zd[:, d - h:d - h + 16, :], T.idb[:, h:128:2], i + h == 0, i + h == 2, [k, "idb"])
-    for b in range(2):
-        for c in range(8):
-            mm(b, P[b][:, c:512:8], T.cb[:, :, :, c], T.idb[:, 64 * b:64 * b + 64], False, c == 7, ["cb", "idb"])
-    edge_in("s", 0, 0, 1)
-    op("v", lambda: V.tensor_tensor_scan(T.rb[:, 1:65], T.ones[:, 0:64], P[4][:, 0:64], 0.0, A.add, A.subtract),
-       ["ones"], ["rb"], [4])
-    tt(T.wf[:, :], P[4][:, 0:64], T.cc[:, :], A.mult, ["cc"], ["wf"], [4])
-    mm(5, P[5][:, 0:64], T.lt[:, :], T.rb[:, 1:65], True, False, ["lt", "rb"])
-    mm(5, P[5][:, 0:64], T.ut[:, :], T.rb[:, 0:64], False, False, ["ut", "rb", "rb0"])
-    mm(5, P[5][:, 0:64], T.idf[:, :], T.wf[:, :], False, True, ["idf", "wf"])
-    for b in range(2):
-        cp("s", T.pay[:, 512 * b:512 * b + 512], P[b][:, :], [], ["pay%d" % b], [b])
-    edge_in("v", 1, 1, 2)
-    cp("v", T.off16[:, :], P[5][:, 0:64], [], ["off16"], [5])
-    edge_mm(0, 1)
-    edge_in("s", 0, 1, 2)
-    edge_mm(0, 0)
-    edge_in("s", 0, 2, 4)
-    edge_mm(1, 0)
-    edge_in("s", 1, 2, 4)
-    edge_mm(1, 1)
-    scatter(0, 48)
-    edge_sum(0)
-    tt(T.tb2[:, :], T.xr[:, :, NB:BW], T.tb[:, :], A.add, ["tb", "arr", "ro"], ["tb2"])
-    edge_idx(0)
-    ts(T.b16[:, :], T.tb2[:, :], 0.0, float(ZU), A.max, A.min, ["tb2"], ["b16"])
-    scatter(48, 64)
-    edge_sum(1)
-    cp("v", T.e16[:, :], T.sw[:, 0:256], ["sw"], ["e16"])
-    edge_idx(1)
-    end_a(0)
-    cp("s", T.sb[:, :], T.sw[:, 0:256], ["sw"], ["sb"])
-    for t in range(16):
-        mm(7, P[7][:, 0:16], T.zz[:, 1, 15 - t:143 - t], T.sb[:, t:256:16], t == 0, t == 15, ["z2", "sb"])
-    end_a(1)
-    end_b(0)
-    ts(T.ti16[:, :], P[7][:, 0:16], 4095.0, None, A.min, None, [], ["ti16"], [7])
-    end_b(1)
-    tt(T.posf[:, :], T.tabw[:, :].indirect(T.ti16[:, :]), T.posc[:, :], A.add,
-       ["tabw", "ti16"] + ["posc%d" % i for i in range(0, len(CHUNKS), 2)], ["posf"])
-    end_a(2)
-    end_a(3)
-    for a, b in spans:
-        cp("s", T.vt[:, NE + NB * a:NE + NB * b], T.us[:, :].indirect(T.b16[:, 8 * a:8 * b]),
-           ["us", "usz0", "usz1", "b16"], ["vb%d" % a])
-    end_b(2)
-    cp("v", T.pos16[:, :], T.posf[:, :], ["posf"], ["pos16"])
-    end_b(3)
+    def tri():
+        sel(T.bd0[:, :], T.ones[:, 0:128], [[-16, 8], [0, 16]], A.is_ge, 0.0, 0, 1, ["ones"], ["bd0"])
+        sel(T.bd[:, :], T.bd0[:, :], [[16, 8], [0, 16]], A.is_ge, 0.0, 15, -1, ["bd0"], ["bd"])
+        sel(T.lt[:, :], T.bd[:, :], [[1, 128]], A.is_gt, 0.0, 0, -1, ["bd"], ["lt"])
+        sel(T.ut[:, :], T.bd[:, :], [[-1, 128]], A.is_ge, 0.0, 0, 1, ["bd"], ["ut"])
+        iota(T.cc[:, :], [[16, 64]], 256, 1, ["cc"])
 
-    VT = ["vt0", "vt1", "vt2", "vt3", "vo", "vz"] + ["vb%d" % a for a, b in spans]
-    m0 = 0
-    for i, c in enumerate(CHUNKS):
-        q, m, w = "vs"[i % 2], slice(m0, m0 + c), slice(16 * m0, 16 * (m0 + c))
-        cp(q, T.ww[:, w], T.vt[:, :].indirect(T.e16[:, m]), VT + ["e16"], ["w%d" % i])
-        cp(q, T.yy[:, w], T.ww[:, w].indirect(T.pos16[:, m]), ["w%d" % i, "pos16"], ["y%d" % i])
+    def active():
+        ts(T.zd[:, 1:17:2, :], P[2][:, 0:64], 1.0, None, A.is_lt, None, ["zd0"], ["d0"], [2])
+        ts(T.zd[:, 19:35:2, :], P[2][:, 0:64], 255.0, None, A.is_ge, None, ["zd1"], ["d1"], [2])
+        cp("v", T.cb[:, :, 14, :], P[2][:, 0:64], [], ["cb"], [2])
+        for i, (d, k) in enumerate(((1, "d0"), (19, "d1"))):
+            for h in range(2):
+                mm(4, P[4][:, 0:64], T.zd[:, d - h:d - h + 16, :], T.idb[:, h:128:2], i + h == 0, i + h == 2, [k, "idb"])
+        for b in range(2):
+            for c in range(8):
+                mm(b, P[b][:, c:512:8], T.cb[:, :, :, c], T.idb[:, 64 * b:64 * b + 64], False, c == 7, ["cb", "idb"])
+
+    def count():
+        op("v", lambda: V.tensor_tensor_scan(T.rb[:, 1:65], T.ones[:, 0:64], P[4][:, 0:64], 0.0, A.add, A.subtract),
+           ["ones", "d1"], ["rb"], [4])
+        tt(T.wf[:, :], P[4][:, 0:64], T.cc[:, :], A.mult, ["cc"], ["wf"], [4])
+        mm(5, P[5][:, 0:64], T.lt[:, :], T.rb[:, 1:65], True, False, ["lt", "rb"])
+        mm(5, P[5][:, 0:64], T.ut[:, :], T.rb[:, 0:64], False, False, ["ut", "rb", "rb0"])
+        mm(5, P[5][:, 0:64], T.idf[:, :], T.wf[:, :], False, True, ["idf", "wf"])
+
+    def scatter(i):
+        cp("v", T.sw[:, :].indirect(T.off16[:, 16 * i:16 * i + 16]), T.pay[:, 256 * i:256 * i + 256],
+           ["off16", "pay%d" % (i // 2)], ["sw"])
+
+    def kinds(q):
+        cp(QS[q], T.sb[:, :], T.sw[:, 0:256], ["sw"], ["sb"])
+        for t in range(16):
+            mm(7, P[7][:, 0:16], T.zz[:, 1, 15 - t:143 - t], T.sb[:, t:256:16], t == 0, t == 15, ["z2", "sb"])
+
+    def table():
+        convert(T.tabb[:, :], T.tab32[:, :], 512, ["tab32"], ["tabb"])
+        for k in range(8):
+            dma("y", "drep", T.tabw[16 * k:16 * k + 16, :], T.tabb[:, :], ["tabb"], ["tabw"] if k == 7 else [])
+
+    def picks():
+        sel(T.zz[:, 2, 0:8], T.zz[:, 2, 8:16], [[-16, 8]], A.not_equal, 256.0, -13, 1, ["zz"], ["z2a"])
+        sel(T.zz[:, 1, 15:143:16], T.zz[:, 2, 0:8], [[-16, 8]], A.not_equal, 1.0, -14, 1, ["z2a"], ["z2"])
+        for i in range(0, len(CHUNKS), 2):
+            iota(T.posc[:, at[i]:at[i + 2]], [[0, 2], [16, CHUNKS[i]]], 1, 0, ["posc%d" % i])
+
+    def vertices(i, q):
+        cp(QS[q], T.ww[:, 16 * at[i]:16 * at[i + 1]], T.vt[:, :].indirect(T.e16[:, at[i]:at[i + 1]]), VT + ["e16"], ["w%d" % i])
+
+    def entries(i, q):
+        w = slice(16 * at[i], 16 * at[i + 1])
+        cp(QS[q], T.yy[:, w], T.ww[:, w].indirect(T.pos16[:, at[i]:at[i + 1]]), ["w%d" % i, "pos16"], ["y%d" % i])
         dma("y", "dy", T.y[:, w], T.yy[:, w], ["y%d" % i], ["out%d" % i])
-        m0 += c
+
+    step = {
+        "c": corner, "m": case_mm, "x": send, "r": rows, "A": active, "N": count, "e": edge_in, "f": edge_mm, "g": edge_sum,
+        "h": edge_idx, "a": end_a, "b": end_b, "s": scatter, "k": kinds, "B": border, "K": kinds_in, "M": kinds_mm, "R": tri,
+        "D": cells_in, "F": flags_out, "X": ends_out, "G": table, "Z": picks, "z": zero, "W": vertices, "y": entries,
+        "C": lambda: dma("g", "dx", T.us[:, PADC:ZU], T.xs[:, :, :], xs, ["us"]),
+        "S": lambda: dma("g", "dr", T.us[:, PADC:ZU], T.xr[:, :, :], ["arr", "ro"], ["us"], accum_op=A.add),
+        "P": lambda: iota(T.sw[:, 0:256], [[0, 256]], NV, 0, ["sw"]),
+        "w": lambda b, q: cp(QS[q], T.inw[:, 512 * b:512 * b + 512], P[b][:, :], [], ["in%d" % b], [b]),
+        "v": lambda: cp("v", T.cor16[:, :], T.cor32[:, :], ["cor32"], ["cor16"]),
+        "u": lambda: cp("v", T.eab16[:, :], T.eab32[:, :], ["eab32"], ["eab16"]),
+        "l": lambda: cp("v", T.e16[:, :], T.sw[:, 0:256], ["sw"], ["e16"]),
+        "t": lambda: tt(T.tb[:, :], T.xs[:, :, NB:BW], T.jc[:, :], A.add, ["fs", "jc"], ["tb"]),
+        "T": lambda: tt(T.tb2[:, :], T.xr[:, :, NB:BW], T.tb[:, :], A.add, ["tb", "arr", "ro"], ["tb2"]),
+        "U": lambda: ts(T.b16[:, :], T.tb2[:, :], 0.0, float(ZU), A.max, A.min, ["tb2"], ["b16"]),
+        "p": lambda b, q: cp(QS[q], T.pay[:, 512 * b:512 * b + 512], P[b][:, :], ["d1"], ["pay%d" % b], [b]),
+        "o": lambda: cp("v", T.off16[:, :], P[5][:, 0:64], ["wf"], ["off16"], [5]),
+        "i": lambda: ts(T.ti16[:, :], P[7][:, 0:16], 4095.0, None, A.min, None, ["sb"], ["ti16"], [7]),
+        "j": lambda: tt(T.posf[:, :], T.tabw[:, :].indirect(T.ti16[:, :]), T.posc[:, :], A.add,
+                        ["tabw", "ti16"] + ["posc%d" % i for i in range(0, len(CHUNKS), 2)], ["posf"]),
+        "J": lambda: cp("v", T.pos16[:, :], T.posf[:, :], ["posf"], ["pos16"]),
+    }
+    for w in PLAN.split():
+        step[w[0]](*[int(c) for c in w[1:]])
     for sem, cnt in total.items():
         need("y", (sem, cnt, {}))

@@ -1,35 +1,47 @@
 from concourse.bass import DstId, RemoteDMATransfer
 from concourse.mybir import AluOpType, ActivationFunctionType
 
-F32, BF, I32, U16 = "float32", "bfloat16", "int32", "uint16"
+F32, BF, F16, I32, U16 = "float32", "bfloat16", "float16", "int32", "uint16"
 NV, NC, NE, NB = 3072, 1024, 2048, 128
 PADC = 16
 ZC = NV + PADC
-BW = NB + 8
-ZU = PADC + 8 * BW
-DUMP = 1664
-CHUNKS = [16, 16, 40, 40, 40, 40, 24, 24, 8, 8]
-PLAN = ("v K w01 w21 w40 w11 w31 w50 D z F c110 c210 c200 X R c410 c711 c611 x r1 C c401 c000 u r0 m2 G c601 P c511 m4 c501 "
-        "S c010 Z t c300 m0 c701 c310 e001 m6 m5 c100 e100 m3 m1 m7 M A e110 e031 N p00 e011 e021 e131 T f00 f01 p11 o s0 g0 "
-        "s1 h0 e121 f10 f11 s3 U s2 a0 a1 g1 l h1 k1 b0 b1 i a2 a3 b2 j B b3 J "
-        "W30 W10 y10 W21 W01 W41 y30 W90 W50 y21 y41 y01 W61 y50 y61 W70 y91 W81 y70 y81")
+MID = 1536
+STEP = 128
+BLK = 8192
+BIG = 4096
+VAL, MT, LO, KW = 0, 80, 336, 344
+Z0, Z1, Z2, ZH, CHW, SW = 80, 224, 368, 512, 672, 3776
+REP = 1536
+PAY = NC + 72
+OUT = [32, 32, 64, 32, 32, 32, 16, 16]
+
+ORDER = {
+    "v": "zero0 ones lw0 pk0 pk1 zero3 gbo bl16 zero1 dhc cor16 gb0 c0 fs zero2 c2 step eab16 c4 c6 dh2 diag0 tb dh1 neg dh3 act case "
+         "tb2 dh0 b16 count xs1 z diag1 pay1 pay0 off diag3 payz scat fwd pk2 clamp sum0 idx0 cell eg sum1 b0 idx1 ti ag b1 b2 b3 "
+         "n0 n1 nt0 nt1 nu0 nu1 y1 n2 n3 nt2 nt3 nu2 y3 nu3 y5",
+    "s": "ldbl ldcor lw2 pad zd wk sq16 gb1 c1 c3 c5 c7 e01a e01b e00a xs0 e00b e10a e10b e11a e11b a0 a1 diag2 a2 a3 sq k0 k1 k2 k3 "
+         "y0 y2 y4 y6 y7",
+    "p": "gbm m0 m1 m2 m3 m4 m5 m7 m6 actm rows0 countm rows1 offm f01 f00 f10 cellm f11 tim bb0 aa0 bb1 aa1 B0 B1 A0 A1 corr "
+         "bb2 B2 bb3 B3 aa2 A2 aa3 A3",
+    "g": "q bd zz0 val mt val2 idb tabb send1 mt2 tab0 bd2 dq zz2 ut zz1 pv0 send2 pv1 pv2 own zzh zzh2 add",
+    "y": "lw1 lw ldtab ldce ldeab ldch rep tabs ldkd rep2 out0 out1 out2 out3 out4 out6 out5 out7",
+}
 
 SBUF = {
-    BF: dict(lvs=[384], fl=[384], inw=[NV], chw=[NV + 2 * PADC], gcor=[8 * NC], gedg=[2 * NE], gb=[1024], xs=[8, BW],
-             xr=[8, BW], cb=[8, 16, 8], kdb=[128], tabb=[512], tabw=[4096], ca=[NE], sb=[256], uu=[128], ones=[144],
-             bs=[8, 128], ks=[8, 128], zz=[3, 144], zd=[36, 8], sel=[8], wk=[8, 8], idb=[128], bd0=[128], bd=[128],
-             lt=[128], ut=[128], rb=[72]),
-    F32: dict(us=[ZU + PADC], pf=[1], j0=[64], jc=[64], dh=[8, 16, 8], vt=[NV + 16], tb=[64], tb2=[64], te=[256],
-              pay=[NC], sw=[DUMP], posf=[256], posc=[256], ww=[4096], yy=[4096], idf=[128], cc=[64], wf=[64]),
-    I32: dict(bl32=[64], cor32=[512], eab32=[256], pi=[1], pr=[1], d32=[64, 12], kd32=[128], tab32=[512]),
-    U16: dict(bl16=[64], blc=[64], cor16=[512], eab16=[256], b16=[64], i16=[256], e16=[256], ti16=[16], pos16=[256],
-              off16=[64]),
+    BF: dict(lw=[NV], zb=[SW + 1792], zd=[36, 8], wk=[8, 8], gcor=[8 * NC], ge0=[NE], ge1=[NE], gb=[1024], fs=[64], fr=[64],
+             xr=[8 * NB], ca=[NE], ones=[272], idb=[128], bd0=[128], bd=[128], ut=[128], rb=[72], dq=[128], z=[80], kc=[KW],
+             q=[192], pk=[128, 13], step=[256], st=[256], cl=[256], at=[256], sq=[256], dg=[7, 128],
+             tabb=[512], tabw=[4096]),
+    F16: dict(et=[256], dh=[8, 16, 8]),
+    F32: dict(vt=[ZC + PADC], tb=[64], tb2=[64], te=[256], cand=[1536], best=[1536], nf=[256], yy=[4096]),
+    I32: dict(bl32=[64], cor32=[512], eab32=[256], d32=[64, 12], pay=[PAY], tab32=[512]),
+    U16: dict(bl16=[64], cor16=[512], eab16=[256], b16=[64], i16=[256], off16=[8], cell16=[16], ti16=[16], n16=[256]),
 }
 SCRATCH = {k: ("sbuf", [128] + s, d) for d, bufs in SBUF.items() for k, s in bufs.items()}
 SCRATCH.update({"p%d" % b: ("psum", [128, 512], F32) for b in range(8)})
 
-SEMAPHORES = ["cv", "cs", "cp", "cg", "dlv", "dbl", "dcor", "deab", "dkd", "dce", "dch", "dtab", "drep",
-              "arr", "left", "dx", "dr", "dy"]
+SEMAPHORES = ["cv", "cs", "cp", "cg", "dpk", "dlw", "dbl", "dcor", "deab", "dkd", "dce", "dch", "dtab", "dtb0", "dtbs", "drep",
+              "arr1", "left1", "arr2", "left2", "dx", "dr", "dy"]
 
 
 def rank_program(g, core, T, topo):
@@ -38,327 +50,403 @@ def rank_program(g, core, T, topo):
         return
     A, AF = AluOpType, ActivationFunctionType
     n = len(T.cores)
-
     Q = {"v": g.vector, "s": g.scalar, "p": g.tensor, "g": g, "y": g.sync}
-    total = {}
-    known = {q: {} for q in Q}
-    writer, readers, bank = {}, {}, {}
-
-    def need(q, tok):
-        sem, cnt, seen = tok
-        if known[q].get(sem, 0) >= cnt:
-            return
-        Q[q].wait_ge(T.sem[sem], cnt)
-        known[q][sem] = cnt
-        for s, c in seen.items():
-            if known[q].get(s, 0) < c:
-                known[q][s] = c
-
-    def order(q, r, w, b):
-        toks = [writer[k] for k in r]
-        for k in w:
-            toks += readers.get(k, []) + ([writer[k]] if k in writer else [])
-        for k in b:
-            toks += [t for o, t in bank.get(k, {}).items() if o != q]
-        best = {}
-        for t in toks:
-            if t[0] not in best or best[t[0]][1] < t[1]:
-                best[t[0]] = t
-        for t in sorted(best.values(), key=lambda t: -len(t[2])):
-            need(q, t)
-
-    def note(q, sem, inc, r, w, b):
-        total[sem] = total.get(sem, 0) + inc
-        tok = (sem, total[sem], dict(known[q]))
-        for k in r:
-            readers.setdefault(k, []).append(tok)
-        for k in w:
-            writer[k] = tok
-            readers[k] = []
-        for k in b:
-            bank.setdefault(k, {})[q] = tok
-
-    def op(q, fn, r=(), w=(), b=()):
-        order(q, r, w, b)
-        fn().then_inc(T.sem["c" + q], 1)
-        note(q, "c" + q, 1, r, w, b)
-
-    def dma(q, sem, out, in_, r=(), w=(), **kw):
-        order(q, r, w, ())
-        Q[q].dma_start(out, in_, **kw).then_inc(T.sem[sem], 16)
-        note(q, sem, 16, r, w, ())
-
-    V, S, QS = g.vector, g.scalar, "vs"
+    V, S = g.vector, g.scalar
     P = [T["p%d" % i] for i in range(8)]
 
+    place = {name: (q, i) for q, names in ORDER.items() for i, name in enumerate(names.split())}
+    calls, writer, readers, bank, step = [], {}, {}, {}, [None]
+
+    def note(fn, r=(), w=(), b=(), sem=None, inc=1):
+        q, at = place[step[0]]
+        deps = {writer[k] for k in r}
+        for k in w:
+            deps |= set(readers.get(k, [])) | ({writer[k]} if k in writer else set())
+        for k in b:
+            deps |= {c for o, c in bank.get(k, {}).items() if o != q}
+        behind = {bank[k][q] for k in b if q in bank.get(k, {})}
+        me = len(calls)
+        calls.append(dict(q=q, fn=fn, deps=deps, behind=behind, sem=sem or "c" + q, inc=inc, name=step[0], at=at))
+        for k in r:
+            readers.setdefault(k, []).append(me)
+        for k in w:
+            writer[k] = me
+            readers[k] = []
+        for k in b:
+            bank.setdefault(k, {})[q] = me
+
+    def named(name):
+        step[0] = name
+
+    def queue():
+        return place[step[0]][0]
+
+    def in_order(fmt, ks):
+        return sorted(ks, key=lambda k: place[fmt % k][1])
+
+    def dma(sem, out, in_, r=(), w=(), **kw):
+        q = Q[queue()]
+        note(lambda: q.dma_start(out, in_, **kw), r, w, sem=sem, inc=16)
+
     def mm(b, out, lhsT, rhs, start, stop, r):
-        op("p", lambda: g.tensor.matmul(out, lhsT, rhs, start, stop), r=r, b=[b])
+        note(lambda: g.tensor.matmul(out, lhsT, rhs, start, stop), r=r, b=[b])
 
     def ts(out, in0, s1, s2, o0, o1, r, w, b=()):
         if o1 is None:
-            op("v", lambda: V.tensor_scalar(out, in0, s1, None, o0), r, w, b)
+            note(lambda: V.tensor_scalar(out, in0, s1, None, o0), r, w, b)
         else:
-            op("v", lambda: V.tensor_scalar(out, in0, s1, s2, o0, o1), r, w, b)
+            note(lambda: V.tensor_scalar(out, in0, s1, s2, o0, o1), r, w, b)
 
     def tt(out, in0, in1, o, r, w, b=()):
-        op("v", lambda: V.tensor_tensor(out, in0, in1, o), r, w, b)
+        note(lambda: V.tensor_tensor(out, in0, in1, o), r, w, b)
 
-    def cp(q, out, in_, r, w, b=()):
-        if q == "v":
-            op("v", lambda: V.tensor_copy(out, in_), r, w, b)
-        else:
-            op("s", lambda: S.activation(out, in_, AF.Copy), r, w, b)
+    def scan(out, d0, d1, first, o0, o1, r, w, b=()):
+        note(lambda: V.tensor_tensor_scan(out, d0, d1, first, o0, o1), r, w, b)
 
-    def scaled(out, in_, f, r, w):
-        op("s", lambda: S.activation(out, in_, AF.Copy, scale=f), r, w)
-
-    def fill(ap, val, w):
-        op("v", lambda: V.memset(ap, val), w=w)
+    def act(out, in_, fn, r, w, b=(), **kw):
+        note(lambda: S.activation(out, in_, fn, **kw), r, w, b)
 
     def sel(out, in_, pat, cmp, fl, base, cm, r, w):
-        op("g", lambda: g.affine_select(out, in_, pat, cmp, fl, base, cm), r, w)
-
-    def convert(out, in_, k, r, w):
-        sel(out, in_, [[0, k]], A.is_ge, 0.0, 0, 0, r, w)
+        note(lambda: g.affine_select(out, in_, pat, cmp, fl, base, cm), r, w)
 
     def iota(out, pat, base, cm, w):
-        op("g", lambda: g.iota(out, pat, base, cm, allow_small_or_imprecise_dtypes=True), w=w)
+        note(lambda: g.iota(out, pat, base, cm, allow_small_or_imprecise_dtypes=True), w=w)
 
-    peers = [q for q in range(n) if q != rank]
-    spans = [(a, b) for a, b in ((0, rank), (rank + 1, n)) if b > a]
+    def cp(out, in_, r, w, b=(), k=None):
+        if queue() == "v":
+            note(lambda: V.tensor_copy(out, in_), r, w, b)
+        elif queue() == "s":
+            act(out, in_, AF.Copy, r, w, b)
+        else:
+            sel(out, in_, [[0, k]], A.is_ge, 0.0, 0, 0, r, w)
 
-    dma("y", "dlv", T.lvs[0:64, :], T.lv[:, :], w=["lvs"])
-    dma("s", "dbl", T.bl32[:, :], T.bl[:, :], w=["bl32"])
-    dma("s", "dcor", T.cor32[:, :], T.cor[:, :], w=["cor32"])
-    dma("s", "dkd", T.kd32[0:64, :], T.kd[:, :], w=["kd32"])
-    for k in range(8):
-        dma("y", "dce", T.d32[:, 8 * k:8 * k + 8, :], T.ce[k, :], w=["d32"] if k == 7 else [])
-    dma("y", "dch", T.chw[:, PADC:ZC], T.ch[:, :], w=["ch"])
-    dma("y", "deab", T.eab32[:, 0:128], T.ea[:, :])
-    dma("y", "deab", T.eab32[:, 128:256], T.eb[:, :], w=["eab32"])
-    dma("y", "dtab", T.tab32[:, :], T.tab[:, :], w=["tab32"])
+    def scaled(out, in_, f, r, w, b=()):
+        if queue() == "v":
+            ts(out, in_, f, None, A.mult, None, r, w, b)
+        else:
+            act(out, in_, AF.Copy, r, w, b, scale=f)
 
-    iota(T.uu[0:64, :], [[-8, 8], [0, 16]], 0, 1, ["uu"])
-    fill(T.ones[:, :], 1.0, ["ones"])
-    fill(T.zz[:, :, :], 0.0, ["zz"])
-    for s in range(8):
-        ts(T.bs[0:64, s, :], T.uu[0:64, :], float(s), None, A.is_equal, None, ["uu"], ["bs%d" % s])
-    sel(T.sel[:, :], T.ones[:, 0:8], [[-16, 8]], A.is_equal, 0.0, 0, 1, ["ones"], ["sel"])
-    op("g", lambda: g.iota(T.pi[:, :], [[0, 1]], 0, 1), w=["pi"])
-    iota(T.j0[:, :], [[BW, 8], [16, 8]], PADC - NV, 0, ["j0"])
-    for ap, w, k in ((T.gb[:, NB * rank:NB * rank + NB], NB, "gbo"), (T.xs[:, rank, 0:NB], NB, "xo"), (T.xr[:, rank, :], BW, "ro"),
-                     (T.chw[:, 0:PADC], PADC, "chz0"), (T.chw[:, ZC:ZC + PADC], PADC, "chz1"), (T.vt[:, NV:NV + 16], 16, "vz"),
-                     (T.vt[:, NE + NB * rank:NE + NB * rank + NB], NB, "vo"), (T.us[:, 0:PADC], PADC, "usz0"),
-                     (T.us[:, ZU:ZU + PADC], PADC, "usz1"), (T.rb[:, 0:1], 1, "rb0"),
-                     (T.zd[:, 0:18, :], 144, "zd0"), (T.zd[:, 18:36, :], 144, "zd1")):
-        scaled(ap, T.ones[:, 0:w], 0.0, ["ones"], [k])
-    for k in range(8):
-        scaled(T.wk[:, k, :], T.sel[:, :], float(2 ** k), ["sel"], ["wk%d" % k])
-    scaled(T.dh[:, :, 0, :], T.ones[:, 0:64], float(NV), ["ones"], ["dh0"])
-    sel(T.idb[:, :], T.ones[:, 0:128], [[-1, 128]], A.is_equal, 0.0, 0, 1, ["ones"], ["idb"])
-    sel(T.idf[:, :], T.ones[:, 0:128], [[-1, 128]], A.is_equal, 0.0, 0, 1, ["ones"], ["idf"])
-    sel(T.zz[:, 0, 15:143:16], T.zz[:, 0, 14:142:16], [[-16, 8]], A.not_equal, float(NV), 0, 1, ["zz"], ["z1"])
-    ts(T.pr[:, :], T.pi[:, :], 15, None, A.bitwise_and, None, ["pi"], ["pr"])
-    fill(T.cb[:, :, :, :], 0.0, ["cb"])
-    cp("v", T.pf[:, :], T.pr[:, :], ["pr"], ["pf"])
+    def shifted(out, in_, f, r, w, b=()):
+        if queue() == "v":
+            ts(out, in_, f, None, A.add, None, r, w, b)
+        else:
+            act(out, in_, AF.Identity, r, w, b, bias=f)
 
-    ts(T.fl[0:64, :], T.lvs[0:64, :], 0.0, None, A.is_lt, None, ["lvs"], ["fl"])
-    for s in range(8):
-        c = 384 * s
-        while c < 384 * s + 384:
-            e = min(384 * s + 384, (c // 512 + 1) * 512)
-            mm(c // 512, P[c // 512][:, c % 512:c % 512 + e - c], T.bs[0:64, s, :], T.fl[0:64, c - 384 * s:e - 384 * s],
-               True, True, ["bs%d" % s, "fl"])
-            c = e
-    cp("v", T.bl16[:, :], T.bl32[:, :], ["bl32"], ["bl16"])
-    ts(T.blc[:, :], T.bl32[:, :], float(PADC), None, A.add, None, ["bl32"], ["blc"])
-    fill(T.dh[:, :, 13:16, :], 0.0, ["dh1"])
-    ts(T.jc[:, :], T.j0[:, :], T.pf[:, :], None, A.add, None, ["j0", "pf"], ["jc"])
-    IN = ["in%d" % b for b in range(6)]
-    CH = ["ch", "chz0", "chz1"]
-    xs = ["fs", "xo"] + ["x%d" % q for q in peers]
-    VT = ["vt0", "vt1", "vt2", "vt3", "vo", "vz"] + ["vb%d" % a for a, b in spans]
-    at = [sum(CHUNKS[:i]) for i in range(len(CHUNKS) + 1)]
-    done, cases = [], []
+    def fill(ap, k, val, w):
+        if queue() == "v":
+            note(lambda: V.memset(ap, val), w=w)
+        else:
+            scaled(ap, T.ones[:, 0:k], val, ["ones"], w)
 
-    def flags_out():
-        gbs = ["z1", "gbo"]
-        for q, lo, hi in (("v", 0, n // 2), ("s", n // 2, n)):
-            for a, b in spans:
-                a, b = max(a, lo), min(b, hi)
-                if b > a:
-                    cp(q, T.gb[:, NB * a:NB * b], T.inw[:, :].indirect(T.bl16[:, 8 * a:8 * b]), IN + ["bl16"], ["gb%d" % a])
-                    gbs.append("gb%d" % a)
+    def row(ap, k, r, keep, fl, key):
+        sel(ap, ap, [[0, k]], A.is_equal if keep else A.not_equal, fl, -r, 1, [key], [key])
+
+    def to_list(b, k, pick, src, r, first=True, last=True):
         for c in range(16):
-            mm(6, P[6][:, 0:64], T.zz[:, 0, 15 - c:143 - c], T.gb[:, c:1024:16], c == 0, c == 15, gbs)
+            mm(b, P[b][:, 0:k], pick(15 - c, 143 - c), src(c, 16 * k, 16), first and c == 0, last and c == 15, r)
 
-    def ends_out():
-        for q in peers:
-            cp("s", T.xs[:, q, 0:NB], T.chw[:, :].indirect(T.blc[:, 8 * q:8 * q + 8]), CH + ["blc"], ["x%d" % q])
-        cp("s", T.xs[:, :, NB:BW], P[6][:, 0:64], [], ["fs"], [6])
+    def part(t, o=0):
+        return lambda a, b, s=1: t[:, o + a:o + b:s]
 
-    def send():
+    nb, z0, z1, z2, zh, chw, sw = [part(T.zb, o) for o in (0, Z0, Z1, Z2, ZH, CHW, SW)]
+    pay, vt = part(T.pay), part(T.vt)
+    CW = chw(0, ZC + PADC)
+    peers = [q for q in range(n) if q != rank]
+    halves = [[(a, b) for a, b in ((lo, min(rank, hi)), (max(rank + 1, lo), hi)) if b > a]
+              for lo, hi in ((0, n // 2), (n // 2, n))]
+
+    def block(t, q):
+        k = t.shape[1] // n
+        return t[:, k * q:k * q + k]
+
+    def send(src, dst, arr, left, r, w):
         far = [q for q in peers if topo.die(T.cores[q]) != topo.die(core)]
         near = [q for q in peers if q not in far]
-        order("g", xs, (), ())
         tr = []
         for q in peers:
             en = topo.engines(core, T.cores[q])
             i = 4 * far.index(q) if q in far else 4 * near.index(q) + 1
             rid, pid, _ = topo.addr(T.cores[q])
             tr.append(RemoteDMATransfer(dst_ids=[DstId(rid=rid, pnc=pid)], dma_engine_mask=(1 << en[i]) | (1 << en[i + 2]),
-                                        remote_sem=T.sem.arr, src=T.xs[:, q, :], dst=T.xr[:, rank, :]))
-        g.remote_dma_fused(tr, local_sem=T.sem.left)
-        for k in ("arr", "left"):
-            total[k] = 2 * len(peers)
-            writer[k] = (k, total[k], {})
+                                        remote_sem=T.sem[arr], src=block(src, q), dst=block(dst, rank)))
+        note(lambda: g.remote_dma_fused(tr, local_sem=T.sem[left]), r, (), sem=left, inc=2 * len(peers))
+        calls[-1]["remote"] = True
+        note(None, (), w, sem=arr, inc=2 * len(peers))
 
-    def border():
-        for a, b in spans:
-            cp("s", T.vt[:, NE + NB * a:NE + NB * b], T.us[:, :].indirect(T.b16[:, 8 * a:8 * b]),
-               ["us", "usz0", "usz1", "b16"], ["vb%d" % a])
+    for c in range(16):
+        named("lw%d" % (c // 8 + 1)); dma("dlw", T.lw[c:128:16, 0:REP], T.lv[:, 0:REP], w=["lw%d" % c])
+    named("lw0"); note(lambda: V.memset(T.lw[:, REP:NV], 0.0), w=["lw"])
+    named("lw"); dma("dlw", T.lw[0:128:16, REP:NV], T.lv[:, REP:NV], w=["lw"])
+    named("ldtab"); dma("dtab", T.tab32[:, :], T.tab[:, :], w=["tab32"])
+    named("ldbl"); dma("dbl", T.bl32[:, :], T.bl[:, :], w=["bl32"])
+    named("ldcor"); dma("dcor", T.cor32[:, :], T.cor[:, :], w=["cor32"])
+    for k in range(8):
+        named("ldce"); dma("dce", T.d32[:, 8 * k:8 * k + 8, :], T.ce[k, :], w=["d32"] if k == 7 else [])
+    named("ldch"); dma("dch", chw(PADC, ZC), T.ch[:, :], w=["ch"])
+    named("ldeab")
+    dma("deab", T.eab32[:, 0:128], T.ea[:, :])
+    dma("deab", T.eab32[:, 128:256], T.eb[:, :], w=["eab32"])
 
-    def edge_in(end, i, q):
-        cp(QS[q], T.gedg[:, NE * end + 512 * i:NE * end + 512 * i + 512],
-           T.inw[:, :].indirect(T.eab16[:, 128 * end + 32 * i:128 * end + 32 * i + 32]), IN + ["eab16"], ["ge%d_%d" % (end, i)])
+    named("ones"); fill(T.ones[:, :], 272, 1.0, ["ones"])
+    for name, a, b, keys in (("zero0", 64, Z1, ["nb0", "zz0"]), ("zero1", Z1, 496, ["zz1", "zz2"]),
+                             ("zero2", 496, CHW + PADC, ["zz2", "zzh", "chz0"]), ("zero3", CHW + ZC, SW + 256, ["chz1", "sw"])):
+        named(name); fill(T.zb[:, a:b], b - a, 0.0, keys)
+    named("zz0"); sel(z0(15, 143, 16), z0(14, 142, 16), [[-16, 8]], A.not_equal, -0.5 * BIG, 0, 1, ["zz0"], ["zz0"])
+    named("idb"); sel(T.idb[:, :], T.ones[:, 0:128], [[-1, 128]], A.is_equal, 0.0, 0, 1, ["ones"], ["idb"])
+    named("wk")
+    for k in range(8):
+        scaled(T.wk[:, k, :], z0(15, 143, 16), 2.0 ** k / BIG, ["zz0"], ["wk%d" % k])
+    named("zd")
+    for h in range(2):
+        fill(T.zd[:, 18 * h:18 * h + 18, :], 144, 0.0, ["zd%d" % h])
+    named("gbo"); fill(block(T.gb, rank), NB, 0.0, ["gbo"])
+    named("dhc"); fill(T.dh[:, :, 12:16, :], 256, 64.0, ["dhc", "case"])
+    named("pad")
+    for ap, k, keys in ((block(T.fr, rank), 8, ["fro"]), (T.rb[:, 0:1], 1, ["rb0"]),
+                        (vt(0, PADC), PADC, ["vz0"]), (vt(ZC, ZC + PADC), PADC, ["vz1"]), (block(T.xr, rank), NB, ["xro"])):
+        fill(ap, k, 0.0, keys)
+    named("payz"); fill(pay(NC, PAY), 0, 0, ["payz"])
+    named("step"); fill(T.step[:, :], 256, 1.0 * STEP, ["step"])
+    named("bd")
+    sel(T.bd0[:, :], T.ones[:, 0:128], [[-16, 8], [0, 16]], A.is_ge, 0.0, 0, 1, ["ones"], ["bd0"])
+    named("bd2")
+    sel(T.bd[:, :], T.bd0[:, :], [[16, 8], [0, 16]], A.is_ge, 0.0, 15, -1, ["bd0"], ["bd"])
+    named("ut")
+    sel(T.ut[:, :], T.bd[:, :], [[1, 128]], A.is_ge, 0.0, 0, -1, ["bd"], ["ut"])
+    named("dq")
+    iota(T.dq[:, :], [[-100, 2], [1, 64]], 17, 0, ["dq"])
+    named("zz1")
+    iota(T.z[:, 65:80], [[1, 15]], 97, 0, ["zc"])
+    cp(z1(15, 143, 16), T.bd[:, 0:128:16], ["bd", "zz1"], ["zz1"], k=8)
+    named("zz2"); sel(z2(15, 143, 16), T.bd[:, 0:128:16], [[-16, 8]], A.not_equal, -16.0 / BLK, -15, 1, ["bd", "zz2"], ["zz2"])
+    named("zzh")
+    sel(zh(144, 152), zh(0, 8), [[-16, 8]], A.not_equal, 256.0, -12, 1, ["zzh"], ["zzh"])
+    named("zzh2")
+    sel(zh(15, 143, 16), zh(144, 152), [[-16, 8]], A.not_equal, 1.0, -13, 1, ["zzh"], ["zzh"])
+    K, pk = T.kc, T.pk
+    named("val")
+    iota(K[0:16, VAL:VAL + 64], [[-BLK, 64]], -65 * BLK, 0, ["val"])
+    iota(K[0:16, VAL + 64:VAL + 80], [[0, 16]], -320 * STEP, 0, ["end"])
+    iota(K[0:16, LO:KW], [[0, KW - LO]], -1, 0, ["lo"])
+    named("val2")
+    row(K[0:16, VAL:VAL + 64], 64, 15, True, 0.0, "val")
+    row(K[0:16, VAL + 64:VAL + 80], 16, 15, False, -133.0 * BLK, "end")
+    row(K[0:16, LO:KW], KW - LO, 15, False, -256.0 * BLK, "lo")
+    named("mt"); iota(K[0:16, MT:LO], [[0, 4], [64, 64]], 0, 0, ["mt"])
+    named("mt2"); row(K[0:16, MT:LO], 256, 14, True, 0.0, "mt")
+    named("rep")
+    for k in range(1, 8):
+        dma("drep", K[16 * k:16 * k + 16, :], K[0:16, :], ["val", "end", "lo", "mt"], ["kc"] if k == 7 else [])
+    for h in range(3):
+        named("pk%d" % h); fill(pk[:, (0, 44, 86)[h]:(44, 86, 128)[h], :], 0, 0.0, ["pk%d" % h])
+    named("q"); iota(T.q[0:16, :], [[0, 16], [2, 12]], -11, 0, ["q"])
+    named("sq16")
+    act(pk[0:16, 0:16, 1:13], T.q[0:16, :], AF.Square, ["q"], ["pk0", "pka", "pkb"], scale=4.0)
+    named("neg"); scaled(pk[0:16, 0:16, 1:7], pk[0:16, 0:16, 1:7], -1.0, ["pka"], ["pka"])
+    named("pv0")
+    row(pk[0:16, 0:16, 7:13], 96, 15, True, 0.0, "pkb")
+    row(pk[0:16, 0:16, 1:7], 96, 15, True, 0.0, "pka")
+    named("pv1")
+    row(pk[0:16, 0:16, 7:13], 96, 14, False, -42.0 * BIG / 64, "pkb")
+    row(pk[0:16, 0:16, 0:7], 112, 14, False, 42.0 * BIG / 64, "pka")
+    named("pv2")
+    for k0, fl, key in ((6, -1.0, "pkb"), (0, 1.0, "pka")):
+        w = pk[0:16, 0:16, 1 + k0:7 + k0]
+        sel(w, w, [[0, 16], [-1, 6]], A.not_equal, fl, -k0, 1, [key], [key])
+    named("rep2")
+    for k in range(1, 8):
+        dma("dpk", pk[16 * k:16 * k + 16, 16 * k:16 * k + 16, :], pk[0:16, 0:16, :], ["pka", "pkb", "pk1", "pk2"], ["pk"] if k == 7 else [])
+    for k in range(7):
+        named("diag%d" % (k // 2))
+        scaled(T.dg[:, k, :], T.idb[:, :], float(BIG * (2 * k - 11 if k < 6 else 1)), ["idb"], ["dg%d" % k])
 
-    def edge_mm(h, end):
+    def flags(out, off, r, w):
+        win, r = T.lw[:, :].indirect(off), r + ["lw", "lw7", "lw15"]
+        if queue() == "v":
+            ts(out, win, 0.0, 2.0, A.is_ge, A.mult, r, w)
+            return 2
+        act(out, win, AF.Sign, r, w, bias=2.0 ** -125, scale=2.0 ** 16)
+        return 1
+
+    named("cor16"); cp(T.cor16[:, :], T.cor32[:, :], ["cor32"], ["cor16"])
+    named("bl16"); cp(T.bl16[:, :], T.bl32[:, :], ["bl32"], ["bl16"])
+    named("eab16"); cp(T.eab16[:, :], T.eab32[:, :], ["eab32"], ["eab16"])
+    CH = ["ch", "chz0", "chz1"]
+
+    gbs, out = ["zz0", "gbo"], {}
+    for h in range(2):
+        named("gb%d" % h)
+        for a, b in halves[h]:
+            out[h] = flags(T.gb[:, NB * a:NB * b], T.bl16[:, 8 * a:8 * b], ["bl16"], ["gb%d" % a])
+            gbs.append("gb%d" % a)
+    named("gbm"); to_list(6, 64, z0, part(T.gb), gbs)
+    named("fs")
+    for h in range(2):
+        shifted(T.fs[:, 32 * h:32 * h + 32], P[6][:, 32 * h:32 * h + 32], 0.5 * BIG * out[h], [], ["fs%d" % h], [6])
+    named("send1"); send(T.fs, T.fr, "arr1", "left1", ["fs0", "fs1"], ["fr"])
+    named("tabb"); cp(T.tabb[:, :], T.tab32[:, :], ["tab32"], ["tabb"], k=512)
+    named("tab0"); dma("dtb0", T.tabw[0:16, :], T.tabb[:, :], ["tabb"], ["tab0"])
+    named("tabs")
+    for k in range(1, 8):
+        dma("dtbs", T.tabw[16 * k:16 * k + 16, :], T.tabw[0:16, :], ["tab0"], ["tabw"] if k == 7 else [])
+    named("tb"); tt(T.tb[:, :], T.fs[:, :], T.bl32[:, :], A.add, ["fs0", "fs1", "bl32"], ["tb"])
+    named("tb2"); tt(T.tb2[:, :], T.fr[:, :], T.tb[:, :], A.add, ["tb", "fr", "fro"], ["tb2"])
+    named("b16"); ts(T.b16[:, :], T.tb2[:, :], float(PADC - BIG), float(ZC), A.add, A.min, ["tb2"], ["b16"])
+    for h in range(2):
+        named("xs%d" % h)
+        for a, b in halves[h]:
+            cp(T.gb[:, NB * a:NB * b], CW.indirect(T.b16[:, 8 * a:8 * b]), CH + ["b16"], ["gb%d" % a])
+    xs = gbs[1:]
+    named("send2"); send(T.gb, T.xr, "arr2", "left2", xs, ["xr"])
+    named("own"); dma("dx", vt(PADC + NE, ZC), T.gb[:, :], xs, ["vb"])
+    named("add"); dma("dr", vt(PADC + NE, ZC), T.xr[:, :], ["xr", "xro"], ["vb"], accum_op=A.add)
+
+    for c in range(8):
+        named("dh%d" % (c // 2))
+        ts(T.dh[:, :, 0:12, c], T.d32[:, c:64:8, :], -1.0 * MID, None, A.add, None, ["d32"], ["dh_%d" % c])
+    ks, off = in_order("m%d", range(8)), 0.0
+    for k in ks:
+        named("c%d" % k)
+        off += 2.0 ** (k - 1) * flags(T.gcor[:, NC * k:NC * k + NC], T.cor16[:, 64 * k:64 * k + 64], ["cor16"], ["gc%d" % k])
+        named("m%d" % k)
+        for c in range(8):
+            mm(2, P[2][:, c:64:8], T.gcor[:, NC * k + c:NC * k + NC:8], T.wk[:, k, :], k == ks[0] and c == 0, k == ks[-1] and c == 7,
+               ["gc%d" % k, "wk%d" % k])
+    named("act")
+    ts(T.zd[:, 1:17:2, :], P[2][:, 0:64], 1.0 - off, None, A.is_lt, None, ["zd0"], ["d0"], [2])
+    ts(T.zd[:, 19:35:2, :], P[2][:, 0:64], 255.0 - off, None, A.is_ge, None, ["zd1"], ["d1"], [2])
+    named("case"); shifted(T.dh[:, :, 13, :], P[2][:, 0:64], off, [], ["case"], [2])
+    named("actm")
+    for i, (d, k) in enumerate(((1, "d0"), (19, "d1"))):
+        for h in range(2):
+            mm(4, P[4][:, 0:64], T.zd[:, d - h:d - h + 16, :], T.idb[:, h:128:2], i + h == 0, i + h == 2, [k, "idb"])
+    for b in range(2):
+        named("rows%d" % b)
+        for c in range(8):
+            mm(b, P[b][:, c:512:8], T.dh[:, :, :, c], T.idb[:, 64 * b:64 * b + 64], True, True,
+               ["dhc", "dh_%d" % c, "case", "idb"])
+        named("pay%d" % b); cp(pay(512 * b, 512 * b + 512), P[b][:, :], [], ["pay%d" % b], [b])
+    named("ldkd"); dma("dkd", T.pay[12:128:16, 0:NC], T.kd[:, :], w=["pay0", "pay1"])
+
+    named("count")
+    scan(T.rb[:, 1:65], T.ones[:, 0:64], P[4][:, 0:64], 0.0, A.add, A.subtract, ["ones"], ["rb"], [4])
+    ts(nb(0, 64), P[4][:, 0:64], -1.0, 1.0 * STEP, A.add, A.mult, [], ["nb"], [4])
+    named("countm")
+    mm(5, P[5][:, 0:65], T.idb[:, :], T.dq[:, 0:65], True, False, ["idb", "dq"])
+    mm(5, P[5][:, 0:65], T.idb[:, :], T.rb[:, 0:65], False, False, ["idb", "rb", "rb0"])
+    mm(5, P[5][:, 0:65], T.bd[:, :], nb(0, 65), False, True, ["bd", "nb", "nb0"])
+    mm(5, P[5][:, 128:192], T.ut[:, :], nb(0, 64), True, True, ["ut", "nb"])
+    named("z")
+    tt(T.z[:, 0:65], P[5][:, 0:65], T.rb[:, 0:65], A.max, ["rb", "rb0"], ["z"], [5])
+    tt(K[:, VAL:VAL + 64], P[5][:, 128:192], K[:, VAL:VAL + 64], A.min, ["kc"], ["val"], [5])
+    named("offm"); to_list(7, 5, z1, part(T.z), ["zz1", "z", "zc"])
+    named("off"); cp(T.off16[:, 0:5], P[7][:, 0:5], [], ["off16"], [7])
+    named("scat")
+    cp(sw(0, 1792).indirect(T.off16[:, 0:5]), K[:, VAL:VAL + 80], ["off16", "val"], ["sw"])
+    named("fwd")
+    scan(T.st[:, :], T.step[:, :], sw(0, 256), 0.0, A.add, A.min, ["step", "sw"], ["st"])
+    named("clamp"); ts(T.cl[:, :], T.st[:, :], K[:, LO:LO + 1], None, A.max, None, ["st", "kc"], ["cl"])
+    named("cellm"); to_list(7, 16, z2, part(T.cl), ["zz2", "cl"])
+    named("cell"); ts(T.cell16[:, :], P[7][:, 0:16], 15.0 - 16 * 65, None, A.add, None, [], ["cell16"], [7])
+    named("eg")
+    tt(T.et[:, :], pay(0, PAY).indirect(T.cell16[:, :]), K[:, MT:LO], A.add, ["pay0", "pay1", "payz", "cell16", "kc"], ["et"])
+    named("tim"); to_list(7, 16, zh, part(T.et), ["zzh", "et"])
+    named("ti"); ts(T.ti16[:, :], P[7][:, 0:16], 4095.0, None, A.min, None, [], ["ti16"], [7])
+    named("ag"); ts(T.at[:, :], T.tabw[:, :].indirect(T.ti16[:, :]), -5.5, None, A.add, None, ["tabw", "ti16"], ["at"])
+    named("sq"); act(T.sq[:, :], T.at[:, :], AF.Square, ["at"], ["sq"])
+    named("corr")
+    mm(5, P[5][:, 0:256], pk[:, :, 0], T.et[:, :], True, False, ["pk", "et"])
+    mm(5, P[5][:, 0:256], T.dg[:, 6, :], T.sq[:, :], False, True, ["dg6", "sq"])
+
+    for h in range(2):
         b = (3, 6)[h]
-        o = NE * end + 1024 * h
-        for c in range(16):
-            mm(b, P[b][:, 0:64], T.zz[:, 0, 15 - c:143 - c], T.gedg[:, o + c:o + 1024:16], h not in done and c == 0,
-               h in done and c == 15, ["z1", "ge%d_%d" % (end, 2 * h), "ge%d_%d" % (end, 2 * h + 1)])
-        done.append(h)
-
-    def edge_sum(h):
-        b = (3, 6)[h]
+        ends, off = in_order("f%d%%d" % h, range(2)), 0.0
+        for end in ends:
+            t, o, e = T["ge%d" % end], 128 * end + 64 * h, "e%d%d" % (h, end)
+            (qa, ia), (qb, ib) = place[e + "a"], place[e + "b"]
+            assert qa == qb
+            parts = ((e + "a", 0, 64),) if ib == ia + 1 else ((e + "a", 0, 32), (e + "b", 32, 32))
+            for name, a, k in parts:
+                named(name)
+                out = flags(t[:, 1024 * h + 16 * a:1024 * h + 16 * (a + k)], T.eab16[:, o + a:o + a + k], ["eab16"], [name])
+            off += 0.5 * BIG * out
+            named("f%d%d" % (h, end))
+            to_list(b, 64, z0, part(t, 1024 * h), ["zz0"] + [p[0] for p in parts], end == ends[0], end == ends[1])
+        named("sum%d" % h)
         for end in range(2):
             tt(T.te[:, 128 * h + 64 * end:128 * h + 64 * end + 64], P[b][:, 0:64],
-               T.eab32[:, 128 * end + 64 * h:128 * end + 64 * h + 64], A.add, ["eab32"], ["te%d_%d" % (h, end)], [b])
+               T.eab32[:, 128 * end + 64 * h:128 * end + 64 * h + 64], A.add, ["eab32"], ["te%d%d" % (h, end)], [b])
+        named("idx%d" % h)
+        ts(T.i16[:, 128 * h:128 * h + 128], T.te[:, 128 * h:128 * h + 128], PADC - BIG + off, float(ZC), A.add, A.min,
+           ["te%d0" % h, "te%d1" % h], ["i16%d" % h])
+        for i in range(2 * h, 2 * h + 2):
+            o = 128 * h + 32 * (i % 2)
+            named("a%d" % i)
+            cp(T.ca[:, 512 * i:512 * i + 512], CW.indirect(T.i16[:, o:o + 32]), CH + ["i16%d" % h], ["ca%d" % i])
+            named("b%d" % i)
+            tt(vt(PADC + 512 * i, PADC + 512 * i + 512), CW.indirect(T.i16[:, o + 64:o + 96]),
+               T.ca[:, 512 * i:512 * i + 512], A.add, CH + ["i16%d" % h, "ca%d" % i], ["vt%d" % i])
 
-    def edge_idx(h):
-        ts(T.i16[:, 128 * h:128 * h + 128], T.te[:, 128 * h:128 * h + 128], float(PADC - NV), float(ZC), A.add, A.min,
-           ["te%d_0" % h, "te%d_1" % h], ["i16_%d" % h])
+    for j in range(4):
+        m, w = slice(64 * j, 64 * j + 64), slice(384 * j, 384 * j + 384)
+        for name, b, k0 in (("B", (2, 4)[j % 2], 6), ("A", j % 2, 0)):
+            named("%s%d" % (name.lower() * 2, j))
+            for i in range(6):
+                mm(b, P[b][:, i:384:6], pk[:, :, 1 + k0 + i], T.et[:, m], i == 0, False, ["pk", "et"])
+            named("%s%d" % (name, j))
+            for i in range(6):
+                d = 5 - i if k0 else i
+                mm(b, P[b][:, i:384:6], T.dg[:, d, :], T.at[:, m], False, i == 5, ["dg%d" % d, "at"])
+        named("k%d" % j); scaled(T.cand[:, w], P[(2, 4)[j % 2]][:, 0:384], -1.0, [], ["cand%d" % j], [(2, 4)[j % 2]])
+        named("n%d" % j)
+        scan(T.best[:, w], P[j % 2][:, 0:384], T.cand[:, w], -1.0e9, A.max, A.max, ["cand%d" % j], ["best%d" % j], [j % 2])
+        named("nt%d" % j)
+        tt(T.nf[:, m], T.best[:, 384 * j + 5:384 * j + 384:6], P[5][:, m], A.subtract, ["best%d" % j], ["nf%d" % j], [5])
+        named("nu%d" % j)
+        ts(T.n16[:, m], T.nf[:, m], float(MID + PADC), float(ZC), A.add, A.min, ["nf%d" % j], ["n%d" % j])
 
-    def end_a(i):
-        o = 128 * (i // 2) + 32 * (i % 2)
-        cp("s", T.ca[:, 512 * i:512 * i + 512], T.chw[:, :].indirect(T.i16[:, o:o + 32]), CH + ["i16_%d" % (i // 2)], ["ca%d" % i])
+    vts = ["vt0", "vt1", "vt2", "vt3", "vb", "vz0", "vz1"]
+    for i in range(len(OUT)):
+        a, b = sum(OUT[:i]), sum(OUT[:i + 1])
+        named("y%d" % i)
+        cp(T.yy[:, 16 * a:16 * b], vt(0, ZC + PADC).indirect(T.n16[:, a:b]),
+           vts + ["n%d" % j for j in range(a // 64, (b + 63) // 64)], ["y%d" % i])
+        named("out%d" % i); dma("dy", T.y[:, 16 * a:16 * b], T.yy[:, 16 * a:16 * b], ["y%d" % i], ["out%d" % i])
 
-    def end_b(i):
-        o = 128 * (i // 2) + 32 * (i % 2) + 64
-        tt(T.vt[:, 512 * i:512 * i + 512], T.chw[:, :].indirect(T.i16[:, o:o + 32]), T.ca[:, 512 * i:512 * i + 512], A.add,
-           CH + ["i16_%d" % (i // 2), "ca%d" % i], ["vt%d" % i])
+    total = {}
+    line = {q: sorted((i for i, c in enumerate(calls) if c["q"] == q), key=lambda i: (calls[i]["at"], i)) for q in Q}
+    for q in Q:
+        for i in line[q]:
+            c = calls[i]
+            total[c["sem"]] = c["cnt"] = total.get(c["sem"], 0) + c["inc"]
+    known = {q: {} for q in Q}
 
-    def corner(k, h, q):
-        cp(QS[q], T.gcor[:, NC * k + 512 * h:NC * k + 512 * h + 512],
-           T.inw[:, :].indirect(T.cor16[:, 64 * k + 32 * h:64 * k + 32 * h + 32]), IN + ["cor16"], ["gc%d_%d" % (k, h)])
+    def need(q, sem, cnt, seen):
+        if known[q].get(sem, 0) < cnt:
+            Q[q].wait_ge(T.sem[sem], cnt)
+            known[q][sem] = cnt
+            for s, k in seen.items():
+                known[q][s] = max(known[q].get(s, 0), k)
 
-    def zero():
-        mm(2, P[2][:, 0:64], T.cb[:, 0, :, :], T.inw[:, 0:64], True, False, ["cb", "in0"])
-        for b in range(2):
-            mm(b, P[b][:, :], T.cb[:, 0, :, :], T.inw[:, 0:512], True, False, ["cb", "in0"])
-
-    def case_mm(k):
-        cases.append(k)
-        for c in range(8):
-            mm(2, P[2][:, c:64:8], T.gcor[:, NC * k + c:NC * k + NC:8], T.wk[:, k, :], False, len(cases) == 8 and c == 7,
-               ["gc%d_0" % k, "gc%d_1" % k, "wk%d" % k])
-
-    def kinds_in():
-        sel(T.ks[0:64, :, :], T.bs[0:64, :, :], [[0, 64], [1, 16]], A.is_equal, 0.0, -13, 0,
-            ["bs%d" % s for s in range(8)], ["ks"])
-        convert(T.kdb[0:64, :], T.kd32[0:64, :], 128, ["kd32"], ["kdb"])
-
-    def kinds_mm():
-        for s in range(8):
-            mm(s // 4, P[s // 4][:, 128 * (s % 4):128 * (s % 4) + 128], T.ks[0:64, s, :], T.kdb[0:64, :], False, False,
-               ["ks", "kdb"])
-
-    def cells_in():
-        for c in range(8):
-            convert(T.dh[:, :, 1:13, c], T.d32[:, c:64:8, :], 96, ["d32"], ["dh_%d" % c])
-
-    def rows(b):
-        for c in range(8):
-            mm(b, P[b][:, c:512:8], T.dh[:, :, :, c], T.idf[:, 64 * b:64 * b + 64], False, False,
-               ["dh0", "dh1", "dh_%d" % c, "idf"])
-
-    def tri():
-        sel(T.bd0[:, :], T.ones[:, 0:128], [[-16, 8], [0, 16]], A.is_ge, 0.0, 0, 1, ["ones"], ["bd0"])
-        sel(T.bd[:, :], T.bd0[:, :], [[16, 8], [0, 16]], A.is_ge, 0.0, 15, -1, ["bd0"], ["bd"])
-        sel(T.lt[:, :], T.bd[:, :], [[1, 128]], A.is_gt, 0.0, 0, -1, ["bd"], ["lt"])
-        sel(T.ut[:, :], T.bd[:, :], [[-1, 128]], A.is_ge, 0.0, 0, 1, ["bd"], ["ut"])
-        iota(T.cc[:, :], [[16, 64]], 256, 1, ["cc"])
-
-    def active():
-        ts(T.zd[:, 1:17:2, :], P[2][:, 0:64], 1.0, None, A.is_lt, None, ["zd0"], ["d0"], [2])
-        ts(T.zd[:, 19:35:2, :], P[2][:, 0:64], 255.0, None, A.is_ge, None, ["zd1"], ["d1"], [2])
-        cp("v", T.cb[:, :, 14, :], P[2][:, 0:64], [], ["cb"], [2])
-        for i, (d, k) in enumerate(((1, "d0"), (19, "d1"))):
-            for h in range(2):
-                mm(4, P[4][:, 0:64], T.zd[:, d - h:d - h + 16, :], T.idb[:, h:128:2], i + h == 0, i + h == 2, [k, "idb"])
-        for b in range(2):
-            for c in range(8):
-                mm(b, P[b][:, c:512:8], T.cb[:, :, :, c], T.idb[:, 64 * b:64 * b + 64], False, c == 7, ["cb", "idb"])
-
-    def count():
-        op("v", lambda: V.tensor_tensor_scan(T.rb[:, 1:65], T.ones[:, 0:64], P[4][:, 0:64], 0.0, A.add, A.subtract),
-           ["ones", "d1"], ["rb"], [4])
-        tt(T.wf[:, :], P[4][:, 0:64], T.cc[:, :], A.mult, ["cc"], ["wf"], [4])
-        mm(5, P[5][:, 0:64], T.lt[:, :], T.rb[:, 1:65], True, False, ["lt", "rb"])
-        mm(5, P[5][:, 0:64], T.ut[:, :], T.rb[:, 0:64], False, False, ["ut", "rb", "rb0"])
-        mm(5, P[5][:, 0:64], T.idf[:, :], T.wf[:, :], False, True, ["idf", "wf"])
-
-    def scatter(i):
-        cp("v", T.sw[:, :].indirect(T.off16[:, 16 * i:16 * i + 16]), T.pay[:, 256 * i:256 * i + 256],
-           ["off16", "pay%d" % (i // 2)], ["sw"])
-
-    def kinds(q):
-        cp(QS[q], T.sb[:, :], T.sw[:, 0:256], ["sw"], ["sb"])
-        for t in range(16):
-            mm(7, P[7][:, 0:16], T.zz[:, 1, 15 - t:143 - t], T.sb[:, t:256:16], t == 0, t == 15, ["z2", "sb"])
-
-    def table():
-        convert(T.tabb[:, :], T.tab32[:, :], 512, ["tab32"], ["tabb"])
-        for k in range(8):
-            dma("y", "drep", T.tabw[16 * k:16 * k + 16, :], T.tabb[:, :], ["tabb"], ["tabw"] if k == 7 else [])
-
-    def picks():
-        sel(T.zz[:, 2, 0:8], T.zz[:, 2, 8:16], [[-16, 8]], A.not_equal, 256.0, -13, 1, ["zz"], ["z2a"])
-        sel(T.zz[:, 1, 15:143:16], T.zz[:, 2, 0:8], [[-16, 8]], A.not_equal, 1.0, -14, 1, ["z2a"], ["z2"])
-        for i in range(0, len(CHUNKS), 2):
-            iota(T.posc[:, at[i]:at[i + 2]], [[0, 2], [16, CHUNKS[i]]], 1, 0, ["posc%d" % i])
-
-    def vertices(i, q):
-        cp(QS[q], T.ww[:, 16 * at[i]:16 * at[i + 1]], T.vt[:, :].indirect(T.e16[:, at[i]:at[i + 1]]), VT + ["e16"], ["w%d" % i])
-
-    def entries(i, q):
-        w = slice(16 * at[i], 16 * at[i + 1])
-        cp(QS[q], T.yy[:, w], T.ww[:, w].indirect(T.pos16[:, at[i]:at[i + 1]]), ["w%d" % i, "pos16"], ["y%d" % i])
-        dma("y", "dy", T.y[:, w], T.yy[:, w], ["y%d" % i], ["out%d" % i])
-
-    step = {
-        "c": corner, "m": case_mm, "x": send, "r": rows, "A": active, "N": count, "e": edge_in, "f": edge_mm, "g": edge_sum,
-        "h": edge_idx, "a": end_a, "b": end_b, "s": scatter, "k": kinds, "B": border, "K": kinds_in, "M": kinds_mm, "R": tri,
-        "D": cells_in, "F": flags_out, "X": ends_out, "G": table, "Z": picks, "z": zero, "W": vertices, "y": entries,
-        "C": lambda: dma("g", "dx", T.us[:, PADC:ZU], T.xs[:, :, :], xs, ["us"]),
-        "S": lambda: dma("g", "dr", T.us[:, PADC:ZU], T.xr[:, :, :], ["arr", "ro"], ["us"], accum_op=A.add),
-        "P": lambda: iota(T.sw[:, 0:256], [[0, 256]], NV, 0, ["sw"]),
-        "w": lambda b, q: cp(QS[q], T.inw[:, 512 * b:512 * b + 512], P[b][:, :], [], ["in%d" % b], [b]),
-        "v": lambda: cp("v", T.cor16[:, :], T.cor32[:, :], ["cor32"], ["cor16"]),
-        "u": lambda: cp("v", T.eab16[:, :], T.eab32[:, :], ["eab32"], ["eab16"]),
-        "l": lambda: cp("v", T.e16[:, :], T.sw[:, 0:256], ["sw"], ["e16"]),
-        "t": lambda: tt(T.tb[:, :], T.xs[:, :, NB:BW], T.jc[:, :], A.add, ["fs", "jc"], ["tb"]),
-        "T": lambda: tt(T.tb2[:, :], T.xr[:, :, NB:BW], T.tb[:, :], A.add, ["tb", "arr", "ro"], ["tb2"]),
-        "U": lambda: ts(T.b16[:, :], T.tb2[:, :], 0.0, float(ZU), A.max, A.min, ["tb2"], ["b16"]),
-        "p": lambda b, q: cp(QS[q], T.pay[:, 512 * b:512 * b + 512], P[b][:, :], ["d1"], ["pay%d" % b], [b]),
-        "o": lambda: cp("v", T.off16[:, :], P[5][:, 0:64], ["wf"], ["off16"], [5]),
-        "i": lambda: ts(T.ti16[:, :], P[7][:, 0:16], 4095.0, None, A.min, None, ["sb"], ["ti16"], [7]),
-        "j": lambda: tt(T.posf[:, :], T.tabw[:, :].indirect(T.ti16[:, :]), T.posc[:, :], A.add,
-                        ["tabw", "ti16"] + ["posc%d" % i for i in range(0, len(CHUNKS), 2)], ["posf"]),
-        "J": lambda: cp("v", T.pos16[:, :], T.posf[:, :], ["posf"], ["pos16"]),
-    }
-    for w in PLAN.split():
-        step[w[0]](*[int(c) for c in w[1:]])
+    left = len(calls)
+    while left:
+        before = left
+        for q in Q:
+            while line[q] and all("seen" in calls[d] for d in calls[line[q][0]]["deps"] | calls[line[q][0]]["behind"]):
+                c = calls[line[q].pop(0)]
+                best = {}
+                for d in c["deps"]:
+                    e = calls[d]
+                    if e["sem"] not in best or best[e["sem"]]["cnt"] < e["cnt"]:
+                        best[e["sem"]] = e
+                for e in sorted(best.values(), key=lambda e: -len(e["seen"])):
+                    need(q, e["sem"], e["cnt"] if e["inc"] == 1 else total[e["sem"]], e["seen"])
+                c["seen"] = dict(known[q]) if c["fn"] else {}
+                if c["fn"]:
+                    ins = c["fn"]()
+                    if "remote" not in c:
+                        ins.then_inc(T.sem[c["sem"]], c["inc"])
+                left -= 1
+        assert left < before, "ORDER has a cycle"
     for sem, cnt in total.items():
-        need("y", (sem, cnt, {}))
+        need("y", sem, cnt, {})

from concourse.bass import DstId, RemoteDMATransfer
from concourse.mybir import AluOpType, ActivationFunctionType

F32, BF, F16, I32, U16 = "float32", "bfloat16", "float16", "int32", "uint16"
NV, NC, NE, NB = 3072, 1024, 2048, 128
PADC = 16
ZC = NV + PADC
MID = 1536
STEP = 128
BLK = 8192
BIG = 4096
VAL, MT, LO, KW = 0, 80, 336, 344
Z0, Z1, Z2, ZH, CHW, SW = 80, 224, 368, 512, 672, 3776
REP = 1536
PAY = NC + 72
OUT = [32, 32, 64, 32, 32, 32, 16, 16]

ORDER = {
    "v": "zero0 ones lw0 pk0 pk1 zero3 gbo bl16 zero1 dhc cor16 gb0 c0 fs zero2 c2 step eab16 c4 c6 dh2 diag0 tb dh1 neg dh3 act case "
         "tb2 dh0 b16 count xs1 z diag1 pay1 pay0 off diag3 payz scat fwd pk2 clamp sum0 idx0 cell eg sum1 b0 idx1 ti ag b1 b2 b3 "
         "n0 n1 nt0 nt1 nu0 nu1 y1 n2 n3 nt2 nt3 nu2 y3 nu3 y5",
    "s": "ldbl ldcor lw2 pad zd wk sq16 gb1 c1 c3 c5 c7 e01a e01b e00a xs0 e00b e10a e10b e11a e11b a0 a1 diag2 a2 a3 sq k0 k1 k2 k3 "
         "y0 y2 y4 y6 y7",
    "p": "gbm m0 m1 m2 m3 m4 m5 m7 m6 actm rows0 countm rows1 offm f01 f00 f10 cellm f11 tim bb0 aa0 bb1 aa1 B0 B1 A0 A1 corr "
         "bb2 B2 bb3 B3 aa2 A2 aa3 A3",
    "g": "q bd zz0 val mt val2 idb tabb send1 mt2 tab0 bd2 dq zz2 ut zz1 pv0 send2 pv1 pv2 own zzh zzh2 add",
    "y": "lw1 lw ldtab ldce ldeab ldch rep tabs ldkd rep2 out0 out1 out2 out3 out4 out6 out5 out7",
}

SBUF = {
    BF: dict(lw=[NV], zb=[SW + 1792], zd=[36, 8], wk=[8, 8], gcor=[8 * NC], ge0=[NE], ge1=[NE], gb=[1024], fs=[64], fr=[64],
             xr=[8 * NB], ca=[NE], ones=[272], idb=[128], bd0=[128], bd=[128], ut=[128], rb=[72], dq=[128], z=[80], kc=[KW],
             q=[192], pk=[128, 13], step=[256], st=[256], cl=[256], at=[256], sq=[256], dg=[7, 128],
             tabb=[512], tabw=[4096]),
    F16: dict(et=[256], dh=[8, 16, 8]),
    F32: dict(vt=[ZC + PADC], tb=[64], tb2=[64], te=[256], cand=[1536], best=[1536], nf=[256], yy=[4096]),
    I32: dict(bl32=[64], cor32=[512], eab32=[256], d32=[64, 12], pay=[PAY], tab32=[512]),
    U16: dict(bl16=[64], cor16=[512], eab16=[256], b16=[64], i16=[256], off16=[8], cell16=[16], ti16=[16], n16=[256]),
}
SCRATCH = {k: ("sbuf", [128] + s, d) for d, bufs in SBUF.items() for k, s in bufs.items()}
SCRATCH.update({"p%d" % b: ("psum", [128, 512], F32) for b in range(8)})

SEMAPHORES = ["cv", "cs", "cp", "cg", "dpk", "dlw", "dbl", "dcor", "deab", "dkd", "dce", "dch", "dtab", "dtb0", "dtbs", "drep",
              "arr1", "left1", "arr2", "left2", "dx", "dr", "dy"]


def rank_program(g, core, T, topo):
    rank = T.rank_of(core)
    if rank is None:
        return
    A, AF = AluOpType, ActivationFunctionType
    n = len(T.cores)
    Q = {"v": g.vector, "s": g.scalar, "p": g.tensor, "g": g, "y": g.sync}
    V, S = g.vector, g.scalar
    P = [T["p%d" % i] for i in range(8)]

    place = {name: (q, i) for q, names in ORDER.items() for i, name in enumerate(names.split())}
    calls, writer, readers, bank, step = [], {}, {}, {}, [None]

    def note(fn, r=(), w=(), b=(), sem=None, inc=1):
        q, at = place[step[0]]
        deps = {writer[k] for k in r}
        for k in w:
            deps |= set(readers.get(k, [])) | ({writer[k]} if k in writer else set())
        for k in b:
            deps |= {c for o, c in bank.get(k, {}).items() if o != q}
        behind = {bank[k][q] for k in b if q in bank.get(k, {})}
        me = len(calls)
        calls.append(dict(q=q, fn=fn, deps=deps, behind=behind, sem=sem or "c" + q, inc=inc, name=step[0], at=at))
        for k in r:
            readers.setdefault(k, []).append(me)
        for k in w:
            writer[k] = me
            readers[k] = []
        for k in b:
            bank.setdefault(k, {})[q] = me

    def named(name):
        step[0] = name

    def queue():
        return place[step[0]][0]

    def in_order(fmt, ks):
        return sorted(ks, key=lambda k: place[fmt % k][1])

    def dma(sem, out, in_, r=(), w=(), **kw):
        q = Q[queue()]
        note(lambda: q.dma_start(out, in_, **kw), r, w, sem=sem, inc=16)

    def mm(b, out, lhsT, rhs, start, stop, r):
        note(lambda: g.tensor.matmul(out, lhsT, rhs, start, stop), r=r, b=[b])

    def ts(out, in0, s1, s2, o0, o1, r, w, b=()):
        if o1 is None:
            note(lambda: V.tensor_scalar(out, in0, s1, None, o0), r, w, b)
        else:
            note(lambda: V.tensor_scalar(out, in0, s1, s2, o0, o1), r, w, b)

    def tt(out, in0, in1, o, r, w, b=()):
        note(lambda: V.tensor_tensor(out, in0, in1, o), r, w, b)

    def scan(out, d0, d1, first, o0, o1, r, w, b=()):
        note(lambda: V.tensor_tensor_scan(out, d0, d1, first, o0, o1), r, w, b)

    def act(out, in_, fn, r, w, b=(), **kw):
        note(lambda: S.activation(out, in_, fn, **kw), r, w, b)

    def sel(out, in_, pat, cmp, fl, base, cm, r, w):
        note(lambda: g.affine_select(out, in_, pat, cmp, fl, base, cm), r, w)

    def iota(out, pat, base, cm, w):
        note(lambda: g.iota(out, pat, base, cm, allow_small_or_imprecise_dtypes=True), w=w)

    def cp(out, in_, r, w, b=(), k=None):
        if queue() == "v":
            note(lambda: V.tensor_copy(out, in_), r, w, b)
        elif queue() == "s":
            act(out, in_, AF.Copy, r, w, b)
        else:
            sel(out, in_, [[0, k]], A.is_ge, 0.0, 0, 0, r, w)

    def scaled(out, in_, f, r, w, b=()):
        if queue() == "v":
            ts(out, in_, f, None, A.mult, None, r, w, b)
        else:
            act(out, in_, AF.Copy, r, w, b, scale=f)

    def shifted(out, in_, f, r, w, b=()):
        if queue() == "v":
            ts(out, in_, f, None, A.add, None, r, w, b)
        else:
            act(out, in_, AF.Identity, r, w, b, bias=f)

    def fill(ap, k, val, w):
        if queue() == "v":
            note(lambda: V.memset(ap, val), w=w)
        else:
            scaled(ap, T.ones[:, 0:k], val, ["ones"], w)

    def row(ap, k, r, keep, fl, key):
        sel(ap, ap, [[0, k]], A.is_equal if keep else A.not_equal, fl, -r, 1, [key], [key])

    def to_list(b, k, pick, src, r, first=True, last=True):
        for c in range(16):
            mm(b, P[b][:, 0:k], pick(15 - c, 143 - c), src(c, 16 * k, 16), first and c == 0, last and c == 15, r)

    def part(t, o=0):
        return lambda a, b, s=1: t[:, o + a:o + b:s]

    nb, z0, z1, z2, zh, chw, sw = [part(T.zb, o) for o in (0, Z0, Z1, Z2, ZH, CHW, SW)]
    pay, vt = part(T.pay), part(T.vt)
    CW = chw(0, ZC + PADC)
    peers = [q for q in range(n) if q != rank]
    halves = [[(a, b) for a, b in ((lo, min(rank, hi)), (max(rank + 1, lo), hi)) if b > a]
              for lo, hi in ((0, n // 2), (n // 2, n))]

    def block(t, q):
        k = t.shape[1] // n
        return t[:, k * q:k * q + k]

    def send(src, dst, arr, left, r, w):
        far = [q for q in peers if topo.die(T.cores[q]) != topo.die(core)]
        near = [q for q in peers if q not in far]
        tr = []
        for q in peers:
            en = topo.engines(core, T.cores[q])
            i = 4 * far.index(q) if q in far else 4 * near.index(q) + 1
            rid, pid, _ = topo.addr(T.cores[q])
            tr.append(RemoteDMATransfer(dst_ids=[DstId(rid=rid, pnc=pid)], dma_engine_mask=(1 << en[i]) | (1 << en[i + 2]),
                                        remote_sem=T.sem[arr], src=block(src, q), dst=block(dst, rank)))
        note(lambda: g.remote_dma_fused(tr, local_sem=T.sem[left]), r, (), sem=left, inc=2 * len(peers))
        calls[-1]["remote"] = True
        note(None, (), w, sem=arr, inc=2 * len(peers))

    for c in range(16):
        named("lw%d" % (c // 8 + 1)); dma("dlw", T.lw[c:128:16, 0:REP], T.lv[:, 0:REP], w=["lw%d" % c])
    named("lw0"); note(lambda: V.memset(T.lw[:, REP:NV], 0.0), w=["lw"])
    named("lw"); dma("dlw", T.lw[0:128:16, REP:NV], T.lv[:, REP:NV], w=["lw"])
    named("ldtab"); dma("dtab", T.tab32[:, :], T.tab[:, :], w=["tab32"])
    named("ldbl"); dma("dbl", T.bl32[:, :], T.bl[:, :], w=["bl32"])
    named("ldcor"); dma("dcor", T.cor32[:, :], T.cor[:, :], w=["cor32"])
    for k in range(8):
        named("ldce"); dma("dce", T.d32[:, 8 * k:8 * k + 8, :], T.ce[k, :], w=["d32"] if k == 7 else [])
    named("ldch"); dma("dch", chw(PADC, ZC), T.ch[:, :], w=["ch"])
    named("ldeab")
    dma("deab", T.eab32[:, 0:128], T.ea[:, :])
    dma("deab", T.eab32[:, 128:256], T.eb[:, :], w=["eab32"])

    named("ones"); fill(T.ones[:, :], 272, 1.0, ["ones"])
    for name, a, b, keys in (("zero0", 64, Z1, ["nb0", "zz0"]), ("zero1", Z1, 496, ["zz1", "zz2"]),
                             ("zero2", 496, CHW + PADC, ["zz2", "zzh", "chz0"]), ("zero3", CHW + ZC, SW + 256, ["chz1", "sw"])):
        named(name); fill(T.zb[:, a:b], b - a, 0.0, keys)
    named("zz0"); sel(z0(15, 143, 16), z0(14, 142, 16), [[-16, 8]], A.not_equal, -0.5 * BIG, 0, 1, ["zz0"], ["zz0"])
    named("idb"); sel(T.idb[:, :], T.ones[:, 0:128], [[-1, 128]], A.is_equal, 0.0, 0, 1, ["ones"], ["idb"])
    named("wk")
    for k in range(8):
        scaled(T.wk[:, k, :], z0(15, 143, 16), 2.0 ** k / BIG, ["zz0"], ["wk%d" % k])
    named("zd")
    for h in range(2):
        fill(T.zd[:, 18 * h:18 * h + 18, :], 144, 0.0, ["zd%d" % h])
    named("gbo"); fill(block(T.gb, rank), NB, 0.0, ["gbo"])
    named("dhc"); fill(T.dh[:, :, 12:16, :], 256, 64.0, ["dhc", "case"])
    named("pad")
    for ap, k, keys in ((block(T.fr, rank), 8, ["fro"]), (T.rb[:, 0:1], 1, ["rb0"]),
                        (vt(0, PADC), PADC, ["vz0"]), (vt(ZC, ZC + PADC), PADC, ["vz1"]), (block(T.xr, rank), NB, ["xro"])):
        fill(ap, k, 0.0, keys)
    named("payz"); fill(pay(NC, PAY), 0, 0, ["payz"])
    named("step"); fill(T.step[:, :], 256, 1.0 * STEP, ["step"])
    named("bd")
    sel(T.bd0[:, :], T.ones[:, 0:128], [[-16, 8], [0, 16]], A.is_ge, 0.0, 0, 1, ["ones"], ["bd0"])
    named("bd2")
    sel(T.bd[:, :], T.bd0[:, :], [[16, 8], [0, 16]], A.is_ge, 0.0, 15, -1, ["bd0"], ["bd"])
    named("ut")
    sel(T.ut[:, :], T.bd[:, :], [[1, 128]], A.is_ge, 0.0, 0, -1, ["bd"], ["ut"])
    named("dq")
    iota(T.dq[:, :], [[-100, 2], [1, 64]], 17, 0, ["dq"])
    named("zz1")
    iota(T.z[:, 65:80], [[1, 15]], 97, 0, ["zc"])
    cp(z1(15, 143, 16), T.bd[:, 0:128:16], ["bd", "zz1"], ["zz1"], k=8)
    named("zz2"); sel(z2(15, 143, 16), T.bd[:, 0:128:16], [[-16, 8]], A.not_equal, -16.0 / BLK, -15, 1, ["bd", "zz2"], ["zz2"])
    named("zzh")
    sel(zh(144, 152), zh(0, 8), [[-16, 8]], A.not_equal, 256.0, -12, 1, ["zzh"], ["zzh"])
    named("zzh2")
    sel(zh(15, 143, 16), zh(144, 152), [[-16, 8]], A.not_equal, 1.0, -13, 1, ["zzh"], ["zzh"])
    K, pk = T.kc, T.pk
    named("val")
    iota(K[0:16, VAL:VAL + 64], [[-BLK, 64]], -65 * BLK, 0, ["val"])
    iota(K[0:16, VAL + 64:VAL + 80], [[0, 16]], -320 * STEP, 0, ["end"])
    iota(K[0:16, LO:KW], [[0, KW - LO]], -1, 0, ["lo"])
    named("val2")
    row(K[0:16, VAL:VAL + 64], 64, 15, True, 0.0, "val")
    row(K[0:16, VAL + 64:VAL + 80], 16, 15, False, -133.0 * BLK, "end")
    row(K[0:16, LO:KW], KW - LO, 15, False, -256.0 * BLK, "lo")
    named("mt"); iota(K[0:16, MT:LO], [[0, 4], [64, 64]], 0, 0, ["mt"])
    named("mt2"); row(K[0:16, MT:LO], 256, 14, True, 0.0, "mt")
    named("rep")
    for k in range(1, 8):
        dma("drep", K[16 * k:16 * k + 16, :], K[0:16, :], ["val", "end", "lo", "mt"], ["kc"] if k == 7 else [])
    for h in range(3):
        named("pk%d" % h); fill(pk[:, (0, 44, 86)[h]:(44, 86, 128)[h], :], 0, 0.0, ["pk%d" % h])
    named("q"); iota(T.q[0:16, :], [[0, 16], [2, 12]], -11, 0, ["q"])
    named("sq16")
    act(pk[0:16, 0:16, 1:13], T.q[0:16, :], AF.Square, ["q"], ["pk0", "pka", "pkb"], scale=4.0)
    named("neg"); scaled(pk[0:16, 0:16, 1:7], pk[0:16, 0:16, 1:7], -1.0, ["pka"], ["pka"])
    named("pv0")
    row(pk[0:16, 0:16, 7:13], 96, 15, True, 0.0, "pkb")
    row(pk[0:16, 0:16, 1:7], 96, 15, True, 0.0, "pka")
    named("pv1")
    row(pk[0:16, 0:16, 7:13], 96, 14, False, -42.0 * BIG / 64, "pkb")
    row(pk[0:16, 0:16, 0:7], 112, 14, False, 42.0 * BIG / 64, "pka")
    named("pv2")
    for k0, fl, key in ((6, -1.0, "pkb"), (0, 1.0, "pka")):
        w = pk[0:16, 0:16, 1 + k0:7 + k0]
        sel(w, w, [[0, 16], [-1, 6]], A.not_equal, fl, -k0, 1, [key], [key])
    named("rep2")
    for k in range(1, 8):
        dma("dpk", pk[16 * k:16 * k + 16, 16 * k:16 * k + 16, :], pk[0:16, 0:16, :], ["pka", "pkb", "pk1", "pk2"], ["pk"] if k == 7 else [])
    for k in range(7):
        named("diag%d" % (k // 2))
        scaled(T.dg[:, k, :], T.idb[:, :], float(BIG * (2 * k - 11 if k < 6 else 1)), ["idb"], ["dg%d" % k])

    def flags(out, off, r, w):
        win, r = T.lw[:, :].indirect(off), r + ["lw", "lw7", "lw15"]
        if queue() == "v":
            ts(out, win, 0.0, 2.0, A.is_ge, A.mult, r, w)
            return 2
        act(out, win, AF.Sign, r, w, bias=2.0 ** -125, scale=2.0 ** 16)
        return 1

    named("cor16"); cp(T.cor16[:, :], T.cor32[:, :], ["cor32"], ["cor16"])
    named("bl16"); cp(T.bl16[:, :], T.bl32[:, :], ["bl32"], ["bl16"])
    named("eab16"); cp(T.eab16[:, :], T.eab32[:, :], ["eab32"], ["eab16"])
    CH = ["ch", "chz0", "chz1"]

    gbs, out = ["zz0", "gbo"], {}
    for h in range(2):
        named("gb%d" % h)
        for a, b in halves[h]:
            out[h] = flags(T.gb[:, NB * a:NB * b], T.bl16[:, 8 * a:8 * b], ["bl16"], ["gb%d" % a])
            gbs.append("gb%d" % a)
    named("gbm"); to_list(6, 64, z0, part(T.gb), gbs)
    named("fs")
    for h in range(2):
        shifted(T.fs[:, 32 * h:32 * h + 32], P[6][:, 32 * h:32 * h + 32], 0.5 * BIG * out[h], [], ["fs%d" % h], [6])
    named("send1"); send(T.fs, T.fr, "arr1", "left1", ["fs0", "fs1"], ["fr"])
    named("tabb"); cp(T.tabb[:, :], T.tab32[:, :], ["tab32"], ["tabb"], k=512)
    named("tab0"); dma("dtb0", T.tabw[0:16, :], T.tabb[:, :], ["tabb"], ["tab0"])
    named("tabs")
    for k in range(1, 8):
        dma("dtbs", T.tabw[16 * k:16 * k + 16, :], T.tabw[0:16, :], ["tab0"], ["tabw"] if k == 7 else [])
    named("tb"); tt(T.tb[:, :], T.fs[:, :], T.bl32[:, :], A.add, ["fs0", "fs1", "bl32"], ["tb"])
    named("tb2"); tt(T.tb2[:, :], T.fr[:, :], T.tb[:, :], A.add, ["tb", "fr", "fro"], ["tb2"])
    named("b16"); ts(T.b16[:, :], T.tb2[:, :], float(PADC - BIG), float(ZC), A.add, A.min, ["tb2"], ["b16"])
    for h in range(2):
        named("xs%d" % h)
        for a, b in halves[h]:
            cp(T.gb[:, NB * a:NB * b], CW.indirect(T.b16[:, 8 * a:8 * b]), CH + ["b16"], ["gb%d" % a])
    xs = gbs[1:]
    named("send2"); send(T.gb, T.xr, "arr2", "left2", xs, ["xr"])
    named("own"); dma("dx", vt(PADC + NE, ZC), T.gb[:, :], xs, ["vb"])
    named("add"); dma("dr", vt(PADC + NE, ZC), T.xr[:, :], ["xr", "xro"], ["vb"], accum_op=A.add)

    for c in range(8):
        named("dh%d" % (c // 2))
        ts(T.dh[:, :, 0:12, c], T.d32[:, c:64:8, :], -1.0 * MID, None, A.add, None, ["d32"], ["dh_%d" % c])
    ks, off = in_order("m%d", range(8)), 0.0
    for k in ks:
        named("c%d" % k)
        off += 2.0 ** (k - 1) * flags(T.gcor[:, NC * k:NC * k + NC], T.cor16[:, 64 * k:64 * k + 64], ["cor16"], ["gc%d" % k])
        named("m%d" % k)
        for c in range(8):
            mm(2, P[2][:, c:64:8], T.gcor[:, NC * k + c:NC * k + NC:8], T.wk[:, k, :], k == ks[0] and c == 0, k == ks[-1] and c == 7,
               ["gc%d" % k, "wk%d" % k])
    named("act")
    ts(T.zd[:, 1:17:2, :], P[2][:, 0:64], 1.0 - off, None, A.is_lt, None, ["zd0"], ["d0"], [2])
    ts(T.zd[:, 19:35:2, :], P[2][:, 0:64], 255.0 - off, None, A.is_ge, None, ["zd1"], ["d1"], [2])
    named("case"); shifted(T.dh[:, :, 13, :], P[2][:, 0:64], off, [], ["case"], [2])
    named("actm")
    for i, (d, k) in enumerate(((1, "d0"), (19, "d1"))):
        for h in range(2):
            mm(4, P[4][:, 0:64], T.zd[:, d - h:d - h + 16, :], T.idb[:, h:128:2], i + h == 0, i + h == 2, [k, "idb"])
    for b in range(2):
        named("rows%d" % b)
        for c in range(8):
            mm(b, P[b][:, c:512:8], T.dh[:, :, :, c], T.idb[:, 64 * b:64 * b + 64], True, True,
               ["dhc", "dh_%d" % c, "case", "idb"])
        named("pay%d" % b); cp(pay(512 * b, 512 * b + 512), P[b][:, :], [], ["pay%d" % b], [b])
    named("ldkd"); dma("dkd", T.pay[12:128:16, 0:NC], T.kd[:, :], w=["pay0", "pay1"])

    named("count")
    scan(T.rb[:, 1:65], T.ones[:, 0:64], P[4][:, 0:64], 0.0, A.add, A.subtract, ["ones"], ["rb"], [4])
    ts(nb(0, 64), P[4][:, 0:64], -1.0, 1.0 * STEP, A.add, A.mult, [], ["nb"], [4])
    named("countm")
    mm(5, P[5][:, 0:65], T.idb[:, :], T.dq[:, 0:65], True, False, ["idb", "dq"])
    mm(5, P[5][:, 0:65], T.idb[:, :], T.rb[:, 0:65], False, False, ["idb", "rb", "rb0"])
    mm(5, P[5][:, 0:65], T.bd[:, :], nb(0, 65), False, True, ["bd", "nb", "nb0"])
    mm(5, P[5][:, 128:192], T.ut[:, :], nb(0, 64), True, True, ["ut", "nb"])
    named("z")
    tt(T.z[:, 0:65], P[5][:, 0:65], T.rb[:, 0:65], A.max, ["rb", "rb0"], ["z"], [5])
    tt(K[:, VAL:VAL + 64], P[5][:, 128:192], K[:, VAL:VAL + 64], A.min, ["kc"], ["val"], [5])
    named("offm"); to_list(7, 5, z1, part(T.z), ["zz1", "z", "zc"])
    named("off"); cp(T.off16[:, 0:5], P[7][:, 0:5], [], ["off16"], [7])
    named("scat")
    cp(sw(0, 1792).indirect(T.off16[:, 0:5]), K[:, VAL:VAL + 80], ["off16", "val"], ["sw"])
    named("fwd")
    scan(T.st[:, :], T.step[:, :], sw(0, 256), 0.0, A.add, A.min, ["step", "sw"], ["st"])
    named("clamp"); ts(T.cl[:, :], T.st[:, :], K[:, LO:LO + 1], None, A.max, None, ["st", "kc"], ["cl"])
    named("cellm"); to_list(7, 16, z2, part(T.cl), ["zz2", "cl"])
    named("cell"); ts(T.cell16[:, :], P[7][:, 0:16], 15.0 - 16 * 65, None, A.add, None, [], ["cell16"], [7])
    named("eg")
    tt(T.et[:, :], pay(0, PAY).indirect(T.cell16[:, :]), K[:, MT:LO], A.add, ["pay0", "pay1", "payz", "cell16", "kc"], ["et"])
    named("tim"); to_list(7, 16, zh, part(T.et), ["zzh", "et"])
    named("ti"); ts(T.ti16[:, :], P[7][:, 0:16], 4095.0, None, A.min, None, [], ["ti16"], [7])
    named("ag"); ts(T.at[:, :], T.tabw[:, :].indirect(T.ti16[:, :]), -5.5, None, A.add, None, ["tabw", "ti16"], ["at"])
    named("sq"); act(T.sq[:, :], T.at[:, :], AF.Square, ["at"], ["sq"])
    named("corr")
    mm(5, P[5][:, 0:256], pk[:, :, 0], T.et[:, :], True, False, ["pk", "et"])
    mm(5, P[5][:, 0:256], T.dg[:, 6, :], T.sq[:, :], False, True, ["dg6", "sq"])

    for h in range(2):
        b = (3, 6)[h]
        ends, off = in_order("f%d%%d" % h, range(2)), 0.0
        for end in ends:
            t, o, e = T["ge%d" % end], 128 * end + 64 * h, "e%d%d" % (h, end)
            (qa, ia), (qb, ib) = place[e + "a"], place[e + "b"]
            assert qa == qb
            parts = ((e + "a", 0, 64),) if ib == ia + 1 else ((e + "a", 0, 32), (e + "b", 32, 32))
            for name, a, k in parts:
                named(name)
                out = flags(t[:, 1024 * h + 16 * a:1024 * h + 16 * (a + k)], T.eab16[:, o + a:o + a + k], ["eab16"], [name])
            off += 0.5 * BIG * out
            named("f%d%d" % (h, end))
            to_list(b, 64, z0, part(t, 1024 * h), ["zz0"] + [p[0] for p in parts], end == ends[0], end == ends[1])
        named("sum%d" % h)
        for end in range(2):
            tt(T.te[:, 128 * h + 64 * end:128 * h + 64 * end + 64], P[b][:, 0:64],
               T.eab32[:, 128 * end + 64 * h:128 * end + 64 * h + 64], A.add, ["eab32"], ["te%d%d" % (h, end)], [b])
        named("idx%d" % h)
        ts(T.i16[:, 128 * h:128 * h + 128], T.te[:, 128 * h:128 * h + 128], PADC - BIG + off, float(ZC), A.add, A.min,
           ["te%d0" % h, "te%d1" % h], ["i16%d" % h])
        for i in range(2 * h, 2 * h + 2):
            o = 128 * h + 32 * (i % 2)
            named("a%d" % i)
            cp(T.ca[:, 512 * i:512 * i + 512], CW.indirect(T.i16[:, o:o + 32]), CH + ["i16%d" % h], ["ca%d" % i])
            named("b%d" % i)
            tt(vt(PADC + 512 * i, PADC + 512 * i + 512), CW.indirect(T.i16[:, o + 64:o + 96]),
               T.ca[:, 512 * i:512 * i + 512], A.add, CH + ["i16%d" % h, "ca%d" % i], ["vt%d" % i])

    for j in range(4):
        m, w = slice(64 * j, 64 * j + 64), slice(384 * j, 384 * j + 384)
        for name, b, k0 in (("B", (2, 4)[j % 2], 6), ("A", j % 2, 0)):
            named("%s%d" % (name.lower() * 2, j))
            for i in range(6):
                mm(b, P[b][:, i:384:6], pk[:, :, 1 + k0 + i], T.et[:, m], i == 0, False, ["pk", "et"])
            named("%s%d" % (name, j))
            for i in range(6):
                d = 5 - i if k0 else i
                mm(b, P[b][:, i:384:6], T.dg[:, d, :], T.at[:, m], False, i == 5, ["dg%d" % d, "at"])
        named("k%d" % j); scaled(T.cand[:, w], P[(2, 4)[j % 2]][:, 0:384], -1.0, [], ["cand%d" % j], [(2, 4)[j % 2]])
        named("n%d" % j)
        scan(T.best[:, w], P[j % 2][:, 0:384], T.cand[:, w], -1.0e9, A.max, A.max, ["cand%d" % j], ["best%d" % j], [j % 2])
        named("nt%d" % j)
        tt(T.nf[:, m], T.best[:, 384 * j + 5:384 * j + 384:6], P[5][:, m], A.subtract, ["best%d" % j], ["nf%d" % j], [5])
        named("nu%d" % j)
        ts(T.n16[:, m], T.nf[:, m], float(MID + PADC), float(ZC), A.add, A.min, ["nf%d" % j], ["n%d" % j])

    vts = ["vt0", "vt1", "vt2", "vt3", "vb", "vz0", "vz1"]
    for i in range(len(OUT)):
        a, b = sum(OUT[:i]), sum(OUT[:i + 1])
        named("y%d" % i)
        cp(T.yy[:, 16 * a:16 * b], vt(0, ZC + PADC).indirect(T.n16[:, a:b]),
           vts + ["n%d" % j for j in range(a // 64, (b + 63) // 64)], ["y%d" % i])
        named("out%d" % i); dma("dy", T.y[:, 16 * a:16 * b], T.yy[:, 16 * a:16 * b], ["y%d" % i], ["out%d" % i])

    total = {}
    line = {q: sorted((i for i, c in enumerate(calls) if c["q"] == q), key=lambda i: (calls[i]["at"], i)) for q in Q}
    for q in Q:
        for i in line[q]:
            c = calls[i]
            total[c["sem"]] = c["cnt"] = total.get(c["sem"], 0) + c["inc"]
    known = {q: {} for q in Q}

    def need(q, sem, cnt, seen):
        if known[q].get(sem, 0) < cnt:
            Q[q].wait_ge(T.sem[sem], cnt)
            known[q][sem] = cnt
            for s, k in seen.items():
                known[q][s] = max(known[q].get(s, 0), k)

    left = len(calls)
    while left:
        before = left
        for q in Q:
            while line[q] and all("seen" in calls[d] for d in calls[line[q][0]]["deps"] | calls[line[q][0]]["behind"]):
                c = calls[line[q].pop(0)]
                best = {}
                for d in c["deps"]:
                    e = calls[d]
                    if e["sem"] not in best or best[e["sem"]]["cnt"] < e["cnt"]:
                        best[e["sem"]] = e
                for e in sorted(best.values(), key=lambda e: -len(e["seen"])):
                    need(q, e["sem"], e["cnt"] if e["inc"] == 1 else total[e["sem"]], e["seen"])
                c["seen"] = dict(known[q]) if c["fn"] else {}
                if c["fn"]:
                    ins = c["fn"]()
                    if "remote" not in c:
                        ins.then_inc(T.sem[c["sem"]], c["inc"])
                left -= 1
        assert left < before, "ORDER has a cycle"
    for sem, cnt in total.items():
        need("y", sem, cnt, {})
